import numpy as np
import ml_dtypes


def mxq(x, axis, fmt="e4m3"):
    dtype, down = {"e4m3": (ml_dtypes.float8_e4m3fn, 7), "e5m2": (ml_dtypes.float8_e5m2, 14)}[fmt]
    v = np.moveaxis(np.asarray(x, np.float32).astype(ml_dtypes.bfloat16).astype(np.float64), axis, -1)
    blocks = v.reshape(v.shape[:-1] + (-1, 32))
    amax = np.abs(blocks).max(-1, keepdims=True)
    byte = np.maximum(np.where(amax > 0, np.frexp(amax)[1] - 1 + 127, 0) - down, 1)
    scale = np.exp2(byte - 127.0)
    codes = (blocks / scale).astype(np.float32).astype(dtype).astype(np.float64)
    return np.moveaxis((codes * scale).reshape(v.shape), -1, axis)


WIDE = False


def mx_kscale(k):
    if not WIDE:
        return np.ones(k)
    levels = np.array([10, -10, 5, -5, 0])
    if k % 512:
        return np.exp2(np.random.permutation(np.resize(levels, k // 32))).repeat(32)
    a = np.empty((k // 512, 16))
    for p in range(k // 512):
        a[p, :8] = np.random.permutation(np.resize(levels, 8))
        for g in range(8):
            far = levels[np.abs(levels - a[p, g]) >= 10]
            a[p, g + 8] = far[np.random.randint(len(far))]
    return np.exp2(a.ravel()).repeat(32)


def f64(x):
    return np.asarray(x).astype(np.float64)


def striped(idx):
    return np.tile(idx.reshape(-1, 16).T, (8, 1)).astype(np.uint16)


def unstriped(offs):
    return offs[:16].T.reshape(-1).astype(np.int64)


E2M1 = np.array([0.0, 0.5, 1.0, 1.5, 2.0, 3.0, 4.0, 6.0, -0.0, -0.5, -1.0, -1.5, -2.0, -3.0, -4.0, -6.0])


def pack_fp4(w):
    k, n = w.shape
    w = f64(np.asarray(w, np.float32).astype(ml_dtypes.bfloat16)).reshape(k // 32, 32, n)
    amax = np.abs(w).max(1)
    mant, ex = np.frexp(amax / 6.0)
    byte = np.clip(np.where(amax > 0, np.where(mant > 0.5, ex, ex - 1) + 127, 1), 1, 254)
    scaled = (w * np.exp2(127.0 - byte)[:, None, :]).reshape(k, n).astype(np.float32)
    c = np.ascontiguousarray(scaled.reshape(k // 512, 128, 4, n).transpose(0, 1, 3, 2)).astype(ml_dtypes.float4_e2m1fn).view(np.uint8) & 0xF
    words = (c[..., 0::2] | (c[..., 1::2] << 4)).reshape(k // 512, 128, 2 * n)
    return np.ascontiguousarray(words), np.ascontiguousarray(byte.astype(np.uint8).reshape(k // 512, 16, n))


def unpack_fp4(words, scales):
    g, _, n = scales.shape
    words = np.ascontiguousarray(words).reshape(g, 128, n, 2)
    nib = np.empty((g, 128, n, 4), np.uint8)
    nib[..., 0::2] = words & 0xF
    nib[..., 1::2] = words >> 4
    vals = E2M1[nib] * np.repeat(np.exp2(scales.astype(np.float64) - 127.0), 8, axis=1)[..., None]
    return vals.transpose(0, 1, 3, 2).reshape(g * 512, n)


def relu(v):
    return np.maximum(v, 0.0)


K, T, S, V, H, N = 1024, 2048, 1024, 512, 512, 256


def setup_inputs():
    n = np.random.standard_normal
    s = mx_kscale(K)[:, None]
    u = mx_kscale(H)
    packed_w2 = pack_fp4(n((H, N)) / np.sqrt(2 * H) / u[:, None])
    packed_w3 = pack_fp4(n((H, N)) / np.sqrt(2 * H) / u[:, None])
    return {
        "xT": (n((K, T)) * s).astype(np.float32),
        "w1": (n((K, H)) / np.sqrt(K) / s * u).astype(np.float32),
        "w2_words": packed_w2[0],
        "w2_scales": packed_w2[1],
        "w3_words": packed_w3[0],
        "w3_scales": packed_w3[1],
        "offs": striped(np.random.permutation(T)[:S]),
        "cen": striped(np.random.permutation(S)[:V]),
        "pos1": striped(np.random.permutation(S)[:V]),
        "pos2": striped(np.random.permutation(S)[:V]),
        "pos3": striped(np.random.permutation(S)[:V]),
        "pos4": striped(np.random.permutation(S)[:V]),
    }


def reference(xT, w1, w2_words, w2_scales, w3_words, w3_scales, offs, cen, pos1, pos2, pos3, pos4):
    xq = mxq(f64(xT)[:, unstriped(offs)], 0, "e4m3")
    h = relu(mxq(f64(w1), 0, "e4m3").T @ xq)
    hc = h[:, unstriped(cen)]
    z = (h[:, unstriped(pos1)] + h[:, unstriped(pos2)] + h[:, unstriped(pos3)] + h[:, unstriped(pos4)]) / 4
    return unpack_fp4(w2_words, w2_scales).T @ mxq(hc, 0, "e4m3") + unpack_fp4(w3_words, w3_scales).T @ mxq(z, 0, "e4m3")

@@ -1,0 +1,269 @@
+from contextlib import ExitStack
+
+import concourse.mybir as mybir
+from concourse.masks import make_identity
+
+K, T, S, V, H, N = 1024, 2048, 1024, 512, 512, 256
+FLOPS = 2 * K * H * S + 2 * 2 * H * N * V
+
+F32 = mybir.dt.float32
+BF16 = mybir.dt.bfloat16
+I32 = mybir.dt.int32
+U32 = mybir.dt.uint32
+U16 = mybir.dt.uint16
+U8 = mybir.dt.uint8
+FP8X4 = mybir.dt.float8_e4m3fn_x4
+FP4X4 = mybir.dt.float4_e2m1fn_x4
+ACT = mybir.ActivationFunctionType
+
+P = 128
+PACK = 4
+HALF = 512
+
+
+def tile_picked_sagecat_mean_e_kernel(tc, xT, w1, w2_words, w2_scales, w3_words, w3_scales, offs, cen, pos1, pos2, pos3, pos4, out):
+    nc = tc.nc
+    with ExitStack() as ctx:
+        lists = ctx.enter_context(tc.tile_pool(name="lists", bufs=1))
+        keep = ctx.enter_context(tc.tile_pool(name="keep", bufs=1))
+        ring = ctx.enter_context(tc.tile_pool(name="ring", bufs=8))
+        psum = ctx.enter_context(tc.psum_pool(name="psum", bufs=1))
+
+        def sb(shape, dtype, name, slot=None):
+            return keep.tile(shape, dtype, name=name, tag=slot or name, align_bytes=64)
+
+        def entries(tile, first, count):
+            return tile[:, first // 16 : (first + count) // 16]
+
+        def quantise(grouped, name, slot=None):
+            width = grouped.shape[1] // PACK
+            codes = sb([P, width], U32, name + "_codes", slot)
+            scales = sb([P, width], U8, name + "_scales")
+            nc.vector.quantize_mx(out=codes[:].bitcast(FP8X4), scales=scales[:], in_=grouped)
+            return codes, scales
+
+        chunks = [(0, 512 * c, 512) for c in range(4)] + [(1, 512 * c, 512) for c in range(3)] + [(1, 1536, 256), (1, 1792, 256)]
+        w1_raw = [sb([P, PACK, H], F32, "w1raw%d" % g) for g in range(2)]
+
+        def load_list(src, name):
+            tile = lists.tile([P, src.shape[1]], U16, name=name)
+            nc.sync.dma_start(tile[:], src)
+            return tile
+
+        raw = []
+        for g, first, count in chunks:
+            tile = sb([P, PACK, count], F32, "x%d_%d" % (g, first))
+            rows = xT[512 * g : 512 * (g + 1), :].rearrange("(p j) t -> p j t", j=PACK)
+            nc.sync.dma_start(out=tile[:], in_=rows[:, :, first : first + count])
+            raw.append(tile)
+            if len(raw) == 2:
+                offs_t = load_list(offs, "offs")
+        for g in range(2):
+            nc.sync.dma_start(out=w1_raw[g][:], in_=w1[512 * g : 512 * (g + 1), :].rearrange("(p j) c -> p j c", j=PACK))
+        pos_t = [load_list(src, "pos%d" % d) for d, src in enumerate((pos1, pos2, pos3, pos4))]
+        cen_t = load_list(cen, "cen")
+
+        last_w = []
+        for name, words, scales in (("w3", w3_words, w3_scales), ("w2", w2_words, w2_scales)):
+            wt = sb([P, 2 * N], U8, name + "_words")
+            st = sb([P, N], U8, name + "_plane")
+            nc.gpsimd.memset(st[:], 0)
+            nc.sync.dma_start(out=wt[:], in_=words[0])
+            last_w.append((wt, st))
+        for (wt, st), scales in zip(last_w, (w3_scales, w2_scales)):
+            for q in range(4):
+                nc.sync.dma_start(out=st[32 * q : 32 * q + 4, :].bitcast(I32), in_=scales[0, 4 * q : 4 * q + 4, :].bitcast(I32))
+
+        ident = sb([P, P], F32, "ident")
+        make_identity(nc, ident[:])
+
+        def flat(t):
+            return t[:].rearrange("p n j -> p (n j)")
+
+        all_words = [sb([P, T], U32, "all_words%d" % g) for g in range(2)]
+        all_bytes = sb([P, T], U8, "all_bytes")
+        nc.gpsimd.memset(all_bytes[:], 0)
+        picked_words = [[None, None], [None, None]]
+
+        for (g, first, count), tile in zip(chunks, raw):
+            grouped = sb([P, count, PACK], BF16, "xg%d_%d" % (g, first))
+            cut = count // 2 if count == 512 else 96
+            dst = grouped[:].rearrange("p (c i) j -> p c j i", i=4)
+            src = tile[:].rearrange("p j (c i) -> p c j i", i=4)
+            nc.scalar.activation(dst[:, 0 : cut // 4], src[:, 0 : cut // 4], ACT.Copy)
+            nc.vector.tensor_copy(dst[:, cut // 4 : count // 4], src[:, cut // 4 : count // 4])
+            nc.vector.quantize_mx(
+                out=all_words[g][:, first : first + count].bitcast(FP8X4),
+                scales=all_bytes[4 * g : P, first : first + count],
+                in_=flat(grouped),
+            )
+            if g == 0 and first + count == T:
+                both = sb([P, S], U32, "picked0")
+                nc.vector.tensor_copy(both[:], all_words[0][:].indirect(offs_t[:]))
+                picked_words[0] = [both[:, 0:HALF], both[:, HALF:S]]
+
+        picked_bytes = sb([P, S], U8, "picked_bytes")
+        nc.vector.tensor_copy(picked_bytes[:], all_bytes[:].indirect(offs_t[:]))
+        w0_grouped = sb([P, PACK, P, PACK], BF16, "w0g")
+        nc.scalar.copy(w0_grouped[:].rearrange("p t m j -> p m j t"), w1_raw[0][:].rearrange("p j (m t) -> p m j t", t=PACK))
+        for s in range(2):
+            if s == 1:
+                w0_codes, w0_scales = quantise(w0_grouped[:].rearrange("p t m j -> p (t m j)"), "w0")
+            half = sb([P, HALF], U32, "picked1%d" % s, "w0g" if s == 1 else None)
+            nc.vector.tensor_copy(half[:], all_words[1][:].indirect(entries(offs_t, HALF * s, HALF)))
+            picked_words[1][s] = half[:]
+
+        def group_w1(first, count):
+            tile = sb([P, count, P, PACK], BF16, "w1g%d" % first)
+            src = w1_raw[1][:].rearrange("p j (m t) -> p m j t", t=PACK)[:, :, :, first : first + count]
+            nc.scalar.copy(tile[:].rearrange("p t m j -> p m j t"), src)
+            return tile[:].rearrange("p t m j -> p (t m j)")
+
+        w1_q = {}
+        codes, scales = quantise(group_w1(0, 1), "w1q0")
+        w1_q[0] = (codes[:], scales[:])
+
+        h = [sb([P, S], F32, "h%d" % t) for t in range(PACK)]
+        banks = {}
+
+        def first_pass(t):
+            for s in range(2):
+                banks[t, s] = psum.tile([P, HALF], F32, name="acc%d%d" % (t % 2, s))
+                nc.tensor.matmul_mx(
+                    out=banks[t, s][:],
+                    lhsT=w0_codes[:, P * t : P * (t + 1)].bitcast(FP8X4),
+                    lhsT_scale=w0_scales[:, P * t : P * (t + 1)],
+                    rhs=picked_words[0][s].bitcast(FP8X4),
+                    rhs_scale=picked_bytes[:, HALF * s : HALF * (s + 1)],
+                    start=True,
+                    stop=False,
+                )
+
+        def second_pass(t):
+            for s in range(2):
+                nc.tensor.matmul_mx(
+                    out=banks[t, s][:],
+                    lhsT=w1_q[t][0].bitcast(FP8X4),
+                    lhsT_scale=w1_q[t][1],
+                    rhs=picked_words[1][s].bitcast(FP8X4),
+                    rhs_scale=picked_bytes[4:P, HALF * s : HALF * (s + 1)],
+                    start=False,
+                    stop=True,
+                )
+                if t == 0:
+                    nc.vector.tensor_scalar_max(h[t][:, HALF * s : HALF * (s + 1)], banks[t, s][:], 0.0)
+                else:
+                    nc.scalar.activation(h[t][:, HALF * s : HALF * (s + 1)], banks[t, s][:], ACT.Relu)
+
+        first_pass(0)
+        first_pass(1)
+        second_pass(0)
+        codes, scales = quantise(group_w1(1, 1), "w1q1")
+        w1_q[1] = (codes[:], scales[:])
+        second_pass(1)
+        codes, scales = quantise(group_w1(2, 2), "w1q2")
+        for t in (2, 3):
+            w1_q[t] = (codes[:, P * (t - 2) : P * (t - 1)], scales[:, P * (t - 2) : P * (t - 1)])
+            first_pass(t)
+            second_pass(t)
+
+        z_turned = [[sb([P, 2, P, 2], BF16, "zt%d%d" % (u, vh)) for vh in range(2)] for u in range(2)]
+        back = [psum.tile([P, 2, 256], F32, name="back%d" % vh) for vh in range(2)]
+
+        def neighbours(t, first, count, bank, slots):
+            u, e = divmod(t, 2)
+            blocks = count // P
+            total = psum.tile([P, blocks, P], F32, name=bank)
+            for d in range(4):
+                if d in slots:
+                    got = sb([P, count], F32, slots[d])
+                else:
+                    got = ring.tile([P, count], F32, name="got")
+                nc.vector.tensor_copy(got[:], h[t][:].indirect(entries(pos_t[d], first, count)))
+                for b in range(blocks):
+                    nc.tensor.matmul(
+                        total[:, b, :], got[:, P * b : P * (b + 1)], ident[:],
+                        start=(d == 0 and b == 0), stop=(d == 3 and b == blocks - 1), is_transpose=True,
+                    )
+            for k in range(blocks // 2):
+                vh = first // 256 + k
+                nc.scalar.activation(z_turned[u][vh][:, :, :, e], total[:, 2 * k : 2 * k + 2, :], ACT.Copy, scale=0.25)
+                if e == 1:
+                    words = z_turned[u][vh][:].rearrange("v b p e -> v (b p e)").bitcast(F32)
+                    for b in range(2):
+                        nc.tensor.transpose(back[vh][:, u, P * b : P * (b + 1)], words[:, P * b : P * (b + 1)], ident[:])
+
+        def group_z(vh):
+            tile = sb([P, 256 * PACK], BF16, "zg%d" % vh)
+            nc.scalar.copy(tile[:].bitcast(F32).rearrange("p (v u) -> p v u", u=2), back[vh][:].rearrange("p u v -> p v u"))
+            return tile
+
+        def own(first, count, after, slot):
+            stage = sb([P, PACK, count], BF16, "cstage%d" % first, after)
+            for t in range(PACK):
+                nc.vector.tensor_copy(stage[:, t, :], h[t][:].indirect(entries(cen_t, first, count)))
+            tile = sb([P, count, PACK], BF16, "cg%d" % first, slot)
+            nc.scalar.copy(tile[:].rearrange("p (c i) j -> p c j i", i=4), stage[:].rearrange("p j (c i) -> p c j i", i=4))
+            return tile
+
+        neighbours(0, 0, V, "sum0", {})
+        neighbours(1, 0, V, "sum1", {})
+        neighbours(2, 0, V, "sum0", {2: "gotA"})
+        c_first = own(0, 256, "gotA", None)
+        neighbours(3, 0, 256, "sum1", {})
+        z_first = group_z(0)
+        neighbours(3, 256, 256, "sum0", {0: "gotB", 2: "gotC"})
+        z_second = group_z(1)
+        c_second = own(256, 128, "gotC", "zt11")
+        c_q = [quantise(flat(c_first), "cq0", "gotB")]
+        z_q = [quantise(z_first[:], "zq0")]
+        tail = sb([P, P, PACK], BF16, "cg384", "zg0")
+
+        def tail_gather(t):
+            nc.vector.tensor_copy(tail[:, :, t], h[t][:].indirect(entries(cen_t, 384, P)))
+
+        tail_gather(0)
+        z_q.append(quantise(z_second[:], "zq1"))
+        tail_gather(1)
+        c_q.append(quantise(flat(c_second), "cq1"))
+        tail_gather(2)
+        tail_gather(3)
+        c_q.append(quantise(flat(tail), "cq2"))
+
+        def operand(pair, first):
+            return pair[0][:, first : first + P].bitcast(FP8X4), pair[1][:, first : first + P]
+
+        z_ops = [operand(z_q[c // 2], P * (c % 2)) for c in range(4)]
+        c_ops = [operand(c_q[0], 0), operand(c_q[0], P), operand(c_q[1], 0), operand(c_q[2], 0)]
+
+        def last_pass(dst, which, mh, ops):
+            wt, st = last_w[which]
+            nc.tensor.matmul_mx(
+                out=dst,
+                lhsT=wt[:, 2 * P * mh : 2 * P * (mh + 1)].bitcast(FP4X4),
+                lhsT_scale=st[:, P * mh : P * (mh + 1)],
+                rhs=ops[0],
+                rhs_scale=ops[1],
+                start=(which == 0),
+                stop=(which == 1),
+            )
+
+        early = [psum.tile([P, 3 * P], F32, name="acc0%d" % mh) for mh in range(2)]
+        late = [psum.tile([P, P], F32, name="acc1%d" % mh) for mh in range(2)]
+        for c in range(3):
+            for mh in range(2):
+                last_pass(early[mh][:, P * c : P * (c + 1)], 0, mh, z_ops[c])
+                last_pass(early[mh][:, P * c : P * (c + 1)], 1, mh, c_ops[c])
+        for mh in range(2):
+            last_pass(late[mh][:], 0, mh, z_ops[3])
+        for mh in range(2):
+            last_pass(late[mh][:], 1, mh, c_ops[3])
+        out_v = out.rearrange("(a p) v -> p a v", p=P)
+        res_early = sb([P, 2, 3 * P], F32, "res_early")
+        for mh in range(2):
+            nc.scalar.copy(res_early[:, mh, :], early[mh][:])
+        nc.sync.dma_start(out=out_v[:, :, 0 : 3 * P], in_=res_early[:])
+        res_late = sb([P, 2, P], F32, "res_late")
+        nc.scalar.copy(res_late[:, 0, :], late[0][:])
+        nc.vector.tensor_copy(res_late[:, 1, :], late[1][:])
+        nc.sync.dma_start(out=out_v[:, :, 3 * P : V], in_=res_late[:])

@@ -83,160 +83,189 @@ def tile_picked_sagecat_mean_e_kernel(tc, xT, w1, w2_words, w2_scales, w3_words,
         all_words = [sb([P, T], U32, "all_words%d" % g) for g in range(2)]
         all_bytes = sb([P, T], U8, "all_bytes")
         nc.gpsimd.memset(all_bytes[:], 0)
-        picked_words = [[None, None], [None, None]]
 
         for (g, first, count), tile in zip(chunks, raw):
             grouped = sb([P, count, PACK], BF16, "xg%d_%d" % (g, first))
-            cut = count // 2 if count == 512 else 96
+            cut = {(0, 1536): 192, (1, 0): 384, (1, 512): 320, (1, 1024): 256, (1, 1536): 160, (1, 1792): 160}.get((g, first), 256)
             dst = grouped[:].rearrange("p (c i) j -> p c j i", i=4)
             src = tile[:].rearrange("p j (c i) -> p c j i", i=4)
             nc.scalar.activation(dst[:, 0 : cut // 4], src[:, 0 : cut // 4], ACT.Copy)
-            nc.vector.tensor_copy(dst[:, cut // 4 : count // 4], src[:, cut // 4 : count // 4])
+            if cut < count:
+                nc.vector.tensor_copy(dst[:, cut // 4 : count // 4], src[:, cut // 4 : count // 4])
             nc.vector.quantize_mx(
                 out=all_words[g][:, first : first + count].bitcast(FP8X4),
                 scales=all_bytes[4 * g : P, first : first + count],
                 in_=flat(grouped),
             )
             if g == 0 and first + count == T:
-                both = sb([P, S], U32, "picked0")
-                nc.vector.tensor_copy(both[:], all_words[0][:].indirect(offs_t[:]))
-                picked_words[0] = [both[:, 0:HALF], both[:, HALF:S]]
+                early_words = sb([P, S], U32, "picked0")
+                nc.vector.tensor_copy(early_words[:], all_words[0][:].indirect(offs_t[:]))
 
         picked_bytes = sb([P, S], U8, "picked_bytes")
         nc.vector.tensor_copy(picked_bytes[:], all_bytes[:].indirect(offs_t[:]))
-        w0_grouped = sb([P, PACK, P, PACK], BF16, "w0g")
-        nc.scalar.copy(w0_grouped[:].rearrange("p t m j -> p m j t"), w1_raw[0][:].rearrange("p j (m t) -> p m j t", t=PACK))
-        for s in range(2):
-            if s == 1:
-                w0_codes, w0_scales = quantise(w0_grouped[:].rearrange("p t m j -> p (t m j)"), "w0")
-            half = sb([P, HALF], U32, "picked1%d" % s, "w0g" if s == 1 else None)
-            nc.vector.tensor_copy(half[:], all_words[1][:].indirect(entries(offs_t, HALF * s, HALF)))
-            picked_words[1][s] = half[:]
+        def group_w1(dst, g, first, count):
+            src = w1_raw[g][:].rearrange("p j (m t) -> p m j t", t=PACK)[:, :, :, first : first + count]
+            nc.scalar.copy(dst.rearrange("p t m j -> p m j t"), src)
 
-        def group_w1(first, count):
-            tile = sb([P, count, P, PACK], BF16, "w1g%d" % first)
-            src = w1_raw[1][:].rearrange("p j (m t) -> p m j t", t=PACK)[:, :, :, first : first + count]
-            nc.scalar.copy(tile[:].rearrange("p t m j -> p m j t"), src)
-            return tile[:].rearrange("p t m j -> p (t m j)")
+        def w1_tile(passes, count, name, slot=None):
+            return sb([P, passes, count, P, PACK], BF16, name, slot)
+
+        def w1_flat(tile):
+            return tile[:].rearrange("p g t m j -> p (g t m j)")
 
         w1_q = {}
-        codes, scales = quantise(group_w1(0, 1), "w1q0")
-        w1_q[0] = (codes[:], scales[:])
+        lead = [w1_tile(1, 1, "w1g_lead%d" % g) for g in range(2)]
+        second = w1_tile(2, 1, "w1g_second")
+        group_w1(lead[0][:, 0], 0, 0, 1)
+        codes, scales = quantise(w1_flat(lead[0]), "w1q_lead0")
+        w1_q[0, 0] = (codes[:], scales[:])
+        group_w1(second[:, 0], 0, 1, 1)
+        spans = ((0, 512), (512, 256), (768, 256))
+        late_words = {}
+
+        def pick(first, count, tile, at):
+            nc.vector.tensor_copy(tile[:, at : at + count], all_words[1][:].indirect(entries(offs_t, first, count)))
+            late_words[first] = tile[:, at : at + count]
+
+        pick(0, HALF, sb([P, HALF], U32, "picked10", "w1g_lead0"), 0)
+        src = w1_raw[1][:].rearrange("p j (m t) -> p m j t", t=PACK)[:, :, :, 0:1]
+        dst = lead[1][:, 0].rearrange("p t m j -> p m j t")
+        nc.scalar.copy(dst[:, 0:48], src[:, 0:48])
+        nc.vector.tensor_copy(dst[:, 48:P], src[:, 48:P])
+        codes, scales = quantise(w1_flat(lead[1]), "w1q_lead1")
+        w1_q[1, 0] = (codes[:], scales[:])
+        upper = sb([P, HALF], U32, "picked11", "w1g_lead1")
+        pick(512, 256, upper, 0)
+        pick(768, 256, upper, 256)
 
         h = [sb([P, S], F32, "h%d" % t) for t in range(PACK)]
-        banks = {}
 
-        def first_pass(t):
-            for s in range(2):
-                banks[t, s] = psum.tile([P, HALF], F32, name="acc%d%d" % (t % 2, s))
-                nc.tensor.matmul_mx(
-                    out=banks[t, s][:],
-                    lhsT=w0_codes[:, P * t : P * (t + 1)].bitcast(FP8X4),
-                    lhsT_scale=w0_scales[:, P * t : P * (t + 1)],
-                    rhs=picked_words[0][s].bitcast(FP8X4),
-                    rhs_scale=picked_bytes[:, HALF * s : HALF * (s + 1)],
-                    start=True,
-                    stop=False,
-                )
-
-        def second_pass(t):
-            for s in range(2):
-                nc.tensor.matmul_mx(
-                    out=banks[t, s][:],
-                    lhsT=w1_q[t][0].bitcast(FP8X4),
-                    lhsT_scale=w1_q[t][1],
-                    rhs=picked_words[1][s].bitcast(FP8X4),
-                    rhs_scale=picked_bytes[4:P, HALF * s : HALF * (s + 1)],
-                    start=False,
-                    stop=True,
-                )
-                if t == 0:
-                    nc.vector.tensor_scalar_max(h[t][:, HALF * s : HALF * (s + 1)], banks[t, s][:], 0.0)
+        def hidden(t):
+            cuts = spans if t == 0 else ((0, HALF), (HALF, HALF))
+            names = ("acc%d0" % (t % 2), "acc%d1" % (t % 2), "sum0")
+            banks = [psum.tile([P, count], F32, name=name) for (first, count), name in zip(cuts, names)]
+            for g in range(2):
+                for (first, count), bank in zip(cuts, banks):
+                    if g == 0:
+                        words = early_words[:, first : first + count]
+                    elif first == 0:
+                        words = late_words[0]
+                    else:
+                        words = upper[:, first - HALF : first - HALF + count]
+                    nc.tensor.matmul_mx(
+                        out=bank[:],
+                        lhsT=w1_q[g, t][0].bitcast(FP8X4),
+                        lhsT_scale=w1_q[g, t][1],
+                        rhs=words.bitcast(FP8X4),
+                        rhs_scale=picked_bytes[4 * g : P, first : first + count],
+                        start=(g == 0),
+                        stop=(g == 1),
+                    )
+            for (first, count), bank in zip(cuts, banks):
+                if t == 0 and first > 0:
+                    nc.vector.tensor_scalar_max(h[t][:, first : first + count], bank[:], 0.0)
                 else:
-                    nc.scalar.activation(h[t][:, HALF * s : HALF * (s + 1)], banks[t, s][:], ACT.Relu)
+                    nc.scalar.activation(h[t][:, first : first + count], bank[:], ACT.Relu)
 
-        first_pass(0)
-        first_pass(1)
-        second_pass(0)
-        codes, scales = quantise(group_w1(1, 1), "w1q1")
-        w1_q[1] = (codes[:], scales[:])
-        second_pass(1)
-        codes, scales = quantise(group_w1(2, 2), "w1q2")
-        for t in (2, 3):
-            w1_q[t] = (codes[:, P * (t - 2) : P * (t - 1)], scales[:, P * (t - 2) : P * (t - 1)])
-            first_pass(t)
-            second_pass(t)
+        hidden(0)
+        group_w1(second[:, 1], 1, 1, 1)
+        codes, scales = quantise(w1_flat(second), "w1q_second")
+        for g in range(2):
+            w1_q[g, 1] = (codes[:, P * g : P * (g + 1)], scales[:, P * g : P * (g + 1)])
+        rest = w1_tile(2, 2, "w1g_rest", "w1g_second")
+        for g in range(2):
+            group_w1(rest[:, g], g, 2, 2)
+        codes, scales = quantise(w1_flat(rest), "w1q_rest")
+        for g in range(2):
+            for t in (2, 3):
+                col = P * (2 * g + t - 2)
+                w1_q[g, t] = (codes[:, col : col + P], scales[:, col : col + P])
+        hidden(1)
+        hidden(2)
+        hidden(3)
 
-        z_turned = [[sb([P, 2, P, 2], BF16, "zt%d%d" % (u, vh)) for vh in range(2)] for u in range(2)]
-        back = [psum.tile([P, 2, 256], F32, name="back%d" % vh) for vh in range(2)]
+        pieces = ((0, 2), (2, 1), (3, 1))
+        z_low = sb([P, 4, P, 2], BF16, "z_low")
+        z_high = {first: sb([P, blocks, P, 2], BF16, "z_high%d" % first) for first, blocks in pieces}
+        back = {first: psum.tile([P, 2, P * blocks], F32, name=name) for (first, blocks), name in zip(pieces, ("back0", "back1", "acc11"))}
 
-        def neighbours(t, first, count, bank, slots):
-            u, e = divmod(t, 2)
-            blocks = count // P
+        held = sb([P, 6, V], F32, "got_held", "w1g_second")
+
+        def add_neighbours(t, first, blocks, bank, slots):
             total = psum.tile([P, blocks, P], F32, name=bank)
             for d in range(4):
-                if d in slots:
-                    got = sb([P, count], F32, slots[d])
+                if 2 <= 4 * t + d < 8:
+                    got = held[:, 4 * t + d - 2, :]
+                elif d in slots:
+                    got = sb([P, P * blocks], F32, slots[d])[:]
                 else:
-                    got = ring.tile([P, count], F32, name="got")
-                nc.vector.tensor_copy(got[:], h[t][:].indirect(entries(pos_t[d], first, count)))
+                    got = ring.tile([P, P * blocks], F32, name="got")[:]
+                nc.vector.tensor_copy(got, h[t][:].indirect(entries(pos_t[d], P * first, P * blocks)))
                 for b in range(blocks):
                     nc.tensor.matmul(
                         total[:, b, :], got[:, P * b : P * (b + 1)], ident[:],
                         start=(d == 0 and b == 0), stop=(d == 3 and b == blocks - 1), is_transpose=True,
                     )
-            for k in range(blocks // 2):
-                vh = first // 256 + k
-                nc.scalar.activation(z_turned[u][vh][:, :, :, e], total[:, 2 * k : 2 * k + 2, :], ACT.Copy, scale=0.25)
-                if e == 1:
-                    words = z_turned[u][vh][:].rearrange("v b p e -> v (b p e)").bitcast(F32)
-                    for b in range(2):
-                        nc.tensor.transpose(back[vh][:, u, P * b : P * (b + 1)], words[:, P * b : P * (b + 1)], ident[:])
+            return total
 
-        def group_z(vh):
-            tile = sb([P, 256 * PACK], BF16, "zg%d" % vh)
-            nc.scalar.copy(tile[:].bitcast(F32).rearrange("p (v u) -> p v u", u=2), back[vh][:].rearrange("p u v -> p v u"))
+        def mean(dst, e, total):
+            nc.scalar.activation(dst[:, :, :, e], total, ACT.Copy, scale=0.25)
+
+        def turn_back(src, u, first, blocks):
+            words = src[:].rearrange("v b p e -> v (b p e)").bitcast(F32)
+            for b in range(blocks):
+                c = first + b
+                home = c if c in back else c - 1
+                nc.tensor.transpose(back[home][:, u, P * (c - home) : P * (c - home + 1)], words[:, P * b : P * (b + 1)], ident[:])
+
+        def group_z(first, blocks):
+            tile = sb([P, P * blocks * PACK], BF16, "zg%d" % first)
+            nc.scalar.copy(tile[:].bitcast(F32).rearrange("p (v u) -> p v u", u=2), back[first][:].rearrange("p u v -> p v u"))
             return tile
 
-        def own(first, count, after, slot):
-            stage = sb([P, PACK, count], BF16, "cstage%d" % first, after)
-            for t in range(PACK):
-                nc.vector.tensor_copy(stage[:, t, :], h[t][:].indirect(entries(cen_t, first, count)))
-            tile = sb([P, count, PACK], BF16, "cg%d" % first, slot)
-            nc.scalar.copy(tile[:].rearrange("p (c i) j -> p c j i", i=4), stage[:].rearrange("p j (c i) -> p c j i", i=4))
-            return tile
+        for t in range(2):
+            mean(z_low, t, add_neighbours(t, 0, 4, "sum%d" % t, {})[:])
+        turn_back(z_low, 0, 0, 4)
+        total = add_neighbours(2, 0, 4, "sum0", {3: "got_third"})
+        for first, blocks in pieces:
+            mean(z_high[first], 0, total[:, first : first + blocks, :])
 
-        neighbours(0, 0, V, "sum0", {})
-        neighbours(1, 0, V, "sum1", {})
-        neighbours(2, 0, V, "sum0", {2: "gotA"})
-        c_first = own(0, 256, "gotA", None)
-        neighbours(3, 0, 256, "sum1", {})
-        z_first = group_z(0)
-        neighbours(3, 256, 256, "sum0", {0: "gotB", 2: "gotC"})
-        z_second = group_z(1)
-        c_second = own(256, 128, "gotC", "zt11")
-        c_q = [quantise(flat(c_first), "cq0", "gotB")]
-        z_q = [quantise(z_first[:], "zq0")]
-        tail = sb([P, P, PACK], BF16, "cg384", "zg0")
+        stage = sb([P, PACK, 3 * P], BF16, "c_stage")
+        for t in range(PACK):
+            nc.vector.tensor_copy(stage[:, t, :], h[t][:].indirect(entries(cen_t, 0, 3 * P)))
+        c_early = sb([P, 3 * P, PACK], BF16, "c_early", "got_third")
+        nc.scalar.copy(c_early[:].rearrange("p (c i) j -> p c j i", i=4), stage[:].rearrange("p j (c i) -> p c j i", i=4))
 
-        def tail_gather(t):
-            nc.vector.tensor_copy(tail[:, :, t], h[t][:].indirect(entries(cen_t, 384, P)))
+        z_grouped = {}
 
-        tail_gather(0)
-        z_q.append(quantise(z_second[:], "zq1"))
-        tail_gather(1)
-        c_q.append(quantise(flat(c_second), "cq1"))
-        tail_gather(2)
-        tail_gather(3)
-        c_q.append(quantise(flat(tail), "cq2"))
+        def finish(first, blocks, total):
+            mean(z_high[first], 1, total)
+            turn_back(z_high[first], 1, first, blocks)
+            z_grouped[first] = group_z(first, blocks)
+
+        total = add_neighbours(3, 0, 3, "sum1", {1: "got0_1", 2: "got0_2"})
+        c_q = [
+            quantise(flat(c_early)[:, 0 : 2 * P * PACK], "cq0", "got0_1"),
+            quantise(flat(c_early)[:, 2 * P * PACK : 3 * P * PACK], "cq2", "got0_2"),
+        ]
+        finish(0, 2, total[:, 0:2, :])
+        finish(2, 1, total[:, 2:3, :])
+        finish(3, 1, add_neighbours(3, 3, 1, "back0", {})[:])
+        z_q = [quantise(z_grouped[0][:], "zq0")]
+        tail = sb([P, P, PACK], BF16, "c_tail", "zg0")
+        for t in range(PACK):
+            nc.vector.tensor_copy(tail[:, :, t], h[t][:].indirect(entries(cen_t, 3 * P, P)))
+        z_q.append(quantise(z_grouped[2][:], "zq2"))
+        z_q.append(quantise(z_grouped[3][:], "zq3"))
+        c_q.append(quantise(flat(tail), "cq3"))
 
         def operand(pair, first):
             return pair[0][:, first : first + P].bitcast(FP8X4), pair[1][:, first : first + P]
 
-        z_ops = [operand(z_q[c // 2], P * (c % 2)) for c in range(4)]
+        z_ops = [operand(z_q[0], 0), operand(z_q[0], P), operand(z_q[1], 0), operand(z_q[2], 0)]
         c_ops = [operand(c_q[0], 0), operand(c_q[0], P), operand(c_q[1], 0), operand(c_q[2], 0)]
 
-        def last_pass(dst, which, mh, ops):
+        def last_pass(dst, which, mh, ops, start):
             wt, st = last_w[which]
             nc.tensor.matmul_mx(
                 out=dst,
@@ -244,26 +273,30 @@ def tile_picked_sagecat_mean_e_kernel(tc, xT, w1, w2_words, w2_scales, w3_words,
                 lhsT_scale=st[:, P * mh : P * (mh + 1)],
                 rhs=ops[0],
                 rhs_scale=ops[1],
-                start=(which == 0),
-                stop=(which == 1),
+                start=start,
+                stop=not start,
             )
 
-        early = [psum.tile([P, 3 * P], F32, name="acc0%d" % mh) for mh in range(2)]
-        late = [psum.tile([P, P], F32, name="acc1%d" % mh) for mh in range(2)]
-        for c in range(3):
-            for mh in range(2):
-                last_pass(early[mh][:, P * c : P * (c + 1)], 0, mh, z_ops[c])
-                last_pass(early[mh][:, P * c : P * (c + 1)], 1, mh, c_ops[c])
-        for mh in range(2):
-            last_pass(late[mh][:], 0, mh, z_ops[3])
-        for mh in range(2):
-            last_pass(late[mh][:], 1, mh, c_ops[3])
         out_v = out.rearrange("(a p) v -> p a v", p=P)
-        res_early = sb([P, 2, 3 * P], F32, "res_early")
+        early = [psum.tile([P, 2, P], F32, name="acc0%d" % mh) for mh in range(2)]
+        late = [psum.tile([P, 2, P], F32, name=name) for name in ("acc10", "sum0")]
         for mh in range(2):
-            nc.scalar.copy(res_early[:, mh, :], early[mh][:])
-        nc.sync.dma_start(out=out_v[:, :, 0 : 3 * P], in_=res_early[:])
-        res_late = sb([P, 2, P], F32, "res_late")
-        nc.scalar.copy(res_late[:, 0, :], late[0][:])
-        nc.vector.tensor_copy(res_late[:, 1, :], late[1][:])
-        nc.sync.dma_start(out=out_v[:, :, 3 * P : V], in_=res_late[:])
+            last_pass(late[mh][:, 0, :], 1, mh, c_ops[2], True)
+        for c in range(2):
+            for mh in range(2):
+                last_pass(early[mh][:, c, :], 1, mh, c_ops[c], True)
+                last_pass(early[mh][:, c, :], 0, mh, z_ops[c], False)
+        res_early = sb([P, 2, 2 * P], F32, "res_early")
+        for mh in range(2):
+            nc.scalar.copy(res_early[:, mh, :], early[mh][:].rearrange("p c v -> p (c v)"))
+        nc.sync.dma_start(out=out_v[:, :, 0 : 2 * P], in_=res_early[:])
+        for mh in range(2):
+            last_pass(late[mh][:, 0, :], 0, mh, z_ops[2], False)
+        for mh in range(2):
+            last_pass(late[mh][:, 1, :], 0, mh, z_ops[3], True)
+        for mh in range(2):
+            last_pass(late[mh][:, 1, :], 1, mh, c_ops[3], False)
+        res_late = sb([P, 2, 2 * P], F32, "res_late")
+        nc.scalar.copy(res_late[:, 0, :], late[0][:].rearrange("p c v -> p (c v)"))
+        nc.vector.tensor_copy(res_late[:, 1, :], late[1][:].rearrange("p c v -> p (c v)"))
+        nc.sync.dma_start(out=out_v[:, :, 2 * P : V], in_=res_late[:])

@@ -42,7 +42,7 @@ def tile_picked_sagecat_mean_e_kernel(tc, xT, w1, w2_words, w2_scales, w3_words,
             nc.vector.quantize_mx(out=codes[:].bitcast(FP8X4), scales=scales[:], in_=grouped)
             return codes, scales
 
-        chunks = [(0, 512 * c, 512) for c in range(4)] + [(1, 512 * c, 512) for c in range(3)] + [(1, 1536, 256), (1, 1792, 256)]
+        loads = [(0, 0, 1024), (0, 1024, 1024)] + [(1, 512 * c, 512) for c in range(3)] + [(1, 1536, 256), (1, 1792, 256)]
         w1_raw = [sb([P, PACK, H], F32, "w1raw%d" % g) for g in range(2)]
 
         def load_list(src, name):
@@ -50,12 +50,14 @@ def tile_picked_sagecat_mean_e_kernel(tc, xT, w1, w2_words, w2_scales, w3_words,
             nc.sync.dma_start(tile[:], src)
             return tile
 
-        raw = []
-        for g, first, count in chunks:
+        chunks, raw = [], []
+        for g, first, count in loads:
             tile = sb([P, PACK, count], F32, "x%d_%d" % (g, first))
             rows = xT[512 * g : 512 * (g + 1), :].rearrange("(p j) t -> p j t", j=PACK)
             nc.sync.dma_start(out=tile[:], in_=rows[:, :, first : first + count])
-            raw.append(tile)
+            for at in range(0, count, HALF):
+                chunks.append((g, first + at, min(count, HALF)))
+                raw.append(tile[:, :, at : at + min(count, HALF)])
             if len(raw) == 2:
                 offs_t = load_list(offs, "offs")
         for g in range(2):
@@ -86,9 +88,9 @@ def tile_picked_sagecat_mean_e_kernel(tc, xT, w1, w2_words, w2_scales, w3_words,
 
         for (g, first, count), tile in zip(chunks, raw):
             grouped = sb([P, count, PACK], BF16, "xg%d_%d" % (g, first))
-            cut = {(0, 1536): 192, (1, 0): 384, (1, 512): 320, (1, 1024): 256, (1, 1536): 160, (1, 1792): 160}.get((g, first), 256)
+            cut = {(1, 0): 512, (1, 512): 384, (1, 1536): 160, (1, 1792): 160}.get((g, first), 256)
             dst = grouped[:].rearrange("p (c i) j -> p c j i", i=4)
-            src = tile[:].rearrange("p j (c i) -> p c j i", i=4)
+            src = tile.rearrange("p j (c i) -> p c j i", i=4)
             nc.scalar.activation(dst[:, 0 : cut // 4], src[:, 0 : cut // 4], ACT.Copy)
             if cut < count:
                 nc.vector.tensor_copy(dst[:, cut // 4 : count // 4], src[:, cut // 4 : count // 4])
@@ -172,7 +174,7 @@ def tile_picked_sagecat_mean_e_kernel(tc, xT, w1, w2_words, w2_scales, w3_words,
         codes, scales = quantise(w1_flat(second), "w1q_second")
         for g in range(2):
             w1_q[g, 1] = (codes[:, P * g : P * (g + 1)], scales[:, P * g : P * (g + 1)])
-        rest = w1_tile(2, 2, "w1g_rest", "w1g_second")
+        rest = w1_tile(2, 2, "w1g_rest")
         for g in range(2):
             group_w1(rest[:, g], g, 2, 2)
         codes, scales = quantise(w1_flat(rest), "w1q_rest")
@@ -187,20 +189,16 @@ def tile_picked_sagecat_mean_e_kernel(tc, xT, w1, w2_words, w2_scales, w3_words,
         pieces = ((0, 2), (2, 1), (3, 1))
         z_low = sb([P, 4, P, 2], BF16, "z_low")
         z_high = {first: sb([P, blocks, P, 2], BF16, "z_high%d" % first) for first, blocks in pieces}
-        back = {first: psum.tile([P, 2, P * blocks], F32, name=name) for (first, blocks), name in zip(pieces, ("back0", "back1", "acc11"))}
-
-        held = sb([P, 6, V], F32, "got_held", "w1g_second")
+        back = [psum.tile([P, 2, 256], F32, name="back%d" % vh) for vh in range(2)]
 
         def add_neighbours(t, first, blocks, bank, slots):
             total = psum.tile([P, blocks, P], F32, name=bank)
             for d in range(4):
-                if 2 <= 4 * t + d < 8:
-                    got = held[:, 4 * t + d - 2, :]
-                elif d in slots:
-                    got = sb([P, P * blocks], F32, slots[d])[:]
+                if d in slots:
+                    got = sb([P, P * blocks], F32, slots[d])
                 else:
-                    got = ring.tile([P, P * blocks], F32, name="got")[:]
-                nc.vector.tensor_copy(got, h[t][:].indirect(entries(pos_t[d], P * first, P * blocks)))
+                    got = ring.tile([P, P * blocks], F32, name="got")
+                nc.vector.tensor_copy(got[:], h[t][:].indirect(entries(pos_t[d], P * first, P * blocks)))
                 for b in range(blocks):
                     nc.tensor.matmul(
                         total[:, b, :], got[:, P * b : P * (b + 1)], ident[:],
@@ -215,47 +213,38 @@ def tile_picked_sagecat_mean_e_kernel(tc, xT, w1, w2_words, w2_scales, w3_words,
             words = src[:].rearrange("v b p e -> v (b p e)").bitcast(F32)
             for b in range(blocks):
                 c = first + b
-                home = c if c in back else c - 1
-                nc.tensor.transpose(back[home][:, u, P * (c - home) : P * (c - home + 1)], words[:, P * b : P * (b + 1)], ident[:])
+                nc.tensor.transpose(back[c // 2][:, u, P * (c % 2) : P * (c % 2 + 1)], words[:, P * b : P * (b + 1)], ident[:])
 
         def group_z(first, blocks):
             tile = sb([P, P * blocks * PACK], BF16, "zg%d" % first)
-            nc.scalar.copy(tile[:].bitcast(F32).rearrange("p (v u) -> p v u", u=2), back[first][:].rearrange("p u v -> p v u"))
+            src = back[first // 2][:, :, P * (first % 2) : P * (first % 2 + blocks)]
+            nc.scalar.copy(tile[:].bitcast(F32).rearrange("p (v u) -> p v u", u=2), src.rearrange("p u v -> p v u"))
             return tile
 
         for t in range(2):
             mean(z_low, t, add_neighbours(t, 0, 4, "sum%d" % t, {})[:])
         turn_back(z_low, 0, 0, 4)
-        total = add_neighbours(2, 0, 4, "sum0", {3: "got_third"})
+        total = add_neighbours(2, 0, 4, "sum0", {})
         for first, blocks in pieces:
             mean(z_high[first], 0, total[:, first : first + blocks, :])
 
         stage = sb([P, PACK, 3 * P], BF16, "c_stage")
         for t in range(PACK):
             nc.vector.tensor_copy(stage[:, t, :], h[t][:].indirect(entries(cen_t, 0, 3 * P)))
-        c_early = sb([P, 3 * P, PACK], BF16, "c_early", "got_third")
+        c_early = sb([P, 3 * P, PACK], BF16, "c_early")
         nc.scalar.copy(c_early[:].rearrange("p (c i) j -> p c j i", i=4), stage[:].rearrange("p j (c i) -> p c j i", i=4))
+        c_q = [quantise(flat(c_early)[:, 0 : 2 * P * PACK], "cq0"), quantise(flat(c_early)[:, 2 * P * PACK : 3 * P * PACK], "cq2")]
 
         z_grouped = {}
-
-        def finish(first, blocks, total):
-            mean(z_high[first], 1, total)
+        for k, (first, blocks) in enumerate(pieces):
+            total = add_neighbours(3, first, blocks, "sum%d" % ((k + 1) % 2), {1: "got_last"} if first == 3 else {})
+            mean(z_high[first], 1, total[:])
             turn_back(z_high[first], 1, first, blocks)
             z_grouped[first] = group_z(first, blocks)
-
-        total = add_neighbours(3, 0, 3, "sum1", {1: "got0_1", 2: "got0_2"})
-        c_q = [
-            quantise(flat(c_early)[:, 0 : 2 * P * PACK], "cq0", "got0_1"),
-            quantise(flat(c_early)[:, 2 * P * PACK : 3 * P * PACK], "cq2", "got0_2"),
-        ]
-        finish(0, 2, total[:, 0:2, :])
-        finish(2, 1, total[:, 2:3, :])
-        finish(3, 1, add_neighbours(3, 3, 1, "back0", {})[:])
-        z_q = [quantise(z_grouped[0][:], "zq0")]
-        tail = sb([P, P, PACK], BF16, "c_tail", "zg0")
+        z_q = [quantise(z_grouped[0][:], "zq0", "got_last"), quantise(z_grouped[2][:], "zq2")]
+        tail = sb([P, P, PACK], BF16, "c_tail", "zg2")
         for t in range(PACK):
             nc.vector.tensor_copy(tail[:, :, t], h[t][:].indirect(entries(cen_t, 3 * P, P)))
-        z_q.append(quantise(z_grouped[2][:], "zq2"))
         z_q.append(quantise(z_grouped[3][:], "zq3"))
         c_q.append(quantise(flat(tail), "cq3"))
 
@@ -265,7 +254,7 @@ def tile_picked_sagecat_mean_e_kernel(tc, xT, w1, w2_words, w2_scales, w3_words,
         z_ops = [operand(z_q[0], 0), operand(z_q[0], P), operand(z_q[1], 0), operand(z_q[2], 0)]
         c_ops = [operand(c_q[0], 0), operand(c_q[0], P), operand(c_q[1], 0), operand(c_q[2], 0)]
 
-        def last_pass(dst, which, mh, ops, start):
+        def last_pass(dst, which, mh, ops):
             wt, st = last_w[which]
             nc.tensor.matmul_mx(
                 out=dst,
@@ -273,30 +262,26 @@ def tile_picked_sagecat_mean_e_kernel(tc, xT, w1, w2_words, w2_scales, w3_words,
                 lhsT_scale=st[:, P * mh : P * (mh + 1)],
                 rhs=ops[0],
                 rhs_scale=ops[1],
-                start=start,
-                stop=not start,
+                start=(which == 0),
+                stop=(which == 1),
             )
 
-        out_v = out.rearrange("(a p) v -> p a v", p=P)
-        early = [psum.tile([P, 2, P], F32, name="acc0%d" % mh) for mh in range(2)]
-        late = [psum.tile([P, 2, P], F32, name=name) for name in ("acc10", "sum0")]
-        for mh in range(2):
-            last_pass(late[mh][:, 0, :], 1, mh, c_ops[2], True)
-        for c in range(2):
+        early = [psum.tile([P, 3 * P], F32, name="acc0%d" % mh) for mh in range(2)]
+        late = [psum.tile([P, P], F32, name="acc1%d" % mh) for mh in range(2)]
+        for c in range(3):
             for mh in range(2):
-                last_pass(early[mh][:, c, :], 1, mh, c_ops[c], True)
-                last_pass(early[mh][:, c, :], 0, mh, z_ops[c], False)
-        res_early = sb([P, 2, 2 * P], F32, "res_early")
+                last_pass(early[mh][:, P * c : P * (c + 1)], 0, mh, z_ops[c])
+                last_pass(early[mh][:, P * c : P * (c + 1)], 1, mh, c_ops[c])
         for mh in range(2):
-            nc.scalar.copy(res_early[:, mh, :], early[mh][:].rearrange("p c v -> p (c v)"))
-        nc.sync.dma_start(out=out_v[:, :, 0 : 2 * P], in_=res_early[:])
+            last_pass(late[mh][:], 0, mh, z_ops[3])
         for mh in range(2):
-            last_pass(late[mh][:, 0, :], 0, mh, z_ops[2], False)
+            last_pass(late[mh][:], 1, mh, c_ops[3])
+        out_v = out.rearrange("(a p) v -> p a v", p=P)
+        res_early = sb([P, 2, 3 * P], F32, "res_early")
         for mh in range(2):
-            last_pass(late[mh][:, 1, :], 0, mh, z_ops[3], True)
-        for mh in range(2):
-            last_pass(late[mh][:, 1, :], 1, mh, c_ops[3], False)
-        res_late = sb([P, 2, 2 * P], F32, "res_late")
-        nc.scalar.copy(res_late[:, 0, :], late[0][:].rearrange("p c v -> p (c v)"))
-        nc.vector.tensor_copy(res_late[:, 1, :], late[1][:].rearrange("p c v -> p (c v)"))
-        nc.sync.dma_start(out=out_v[:, :, 2 * P : V], in_=res_late[:])
+            nc.scalar.copy(res_early[:, mh, :], early[mh][:])
+        nc.sync.dma_start(out=out_v[:, :, 0 : 3 * P], in_=res_early[:])
+        res_late = sb([P, 2, P], F32, "res_late")
+        nc.scalar.copy(res_late[:, 0, :], late[0][:])
+        nc.vector.tensor_copy(res_late[:, 1, :], late[1][:])
+        nc.sync.dma_start(out=out_v[:, :, 3 * P : V], in_=res_late[:])

@@ -20,6 +20,9 @@ P = 128
 PACK = 4
 HALF = 512
 
+LOADS = ((0, 0, 1024), (0, 1024, 1024), (1, 0, 512), (1, 512, 512), (1, 1024, 512), (1, 1536, 256), (1, 1792, 256))
+SCALAR_NODES = (320, 320, 256, 256, 512, 384, 320, 144, 128)
+
 
 def tile_picked_sagecat_mean_e_kernel(tc, xT, w1, w2_words, w2_scales, w3_words, w3_scales, offs, cen, pos1, pos2, pos3, pos4, out):
     nc = tc.nc
@@ -32,8 +35,14 @@ def tile_picked_sagecat_mean_e_kernel(tc, xT, w1, w2_words, w2_scales, w3_words,
         def sb(shape, dtype, name, slot=None):
             return keep.tile(shape, dtype, name=name, tag=slot or name, align_bytes=64)
 
+        def bank(shape, slot):
+            return psum.tile(shape, F32, name=slot)
+
         def entries(tile, first, count):
             return tile[:, first // 16 : (first + count) // 16]
+
+        def flat(tile):
+            return tile[:].rearrange("p n j -> p (n j)")
 
         def quantise(grouped, name, slot=None):
             width = grouped.shape[1] // PACK
@@ -42,24 +51,22 @@ def tile_picked_sagecat_mean_e_kernel(tc, xT, w1, w2_words, w2_scales, w3_words,
             nc.vector.quantize_mx(out=codes[:].bitcast(FP8X4), scales=scales[:], in_=grouped)
             return codes, scales
 
-        loads = [(0, 0, 1024), (0, 1024, 1024)] + [(1, 512 * c, 512) for c in range(3)] + [(1, 1536, 256), (1, 1792, 256)]
-        w1_raw = [sb([P, PACK, H], F32, "w1raw%d" % g) for g in range(2)]
-
         def load_list(src, name):
             tile = lists.tile([P, src.shape[1]], U16, name=name)
             nc.sync.dma_start(tile[:], src)
             return tile
 
-        chunks, raw = [], []
-        for g, first, count in loads:
+        pieces = []
+        for g, first, count in LOADS:
             tile = sb([P, PACK, count], F32, "x%d_%d" % (g, first))
             rows = xT[512 * g : 512 * (g + 1), :].rearrange("(p j) t -> p j t", j=PACK)
             nc.sync.dma_start(out=tile[:], in_=rows[:, :, first : first + count])
-            for at in range(0, count, HALF):
-                chunks.append((g, first + at, min(count, HALF)))
-                raw.append(tile[:, :, at : at + min(count, HALF)])
-            if len(raw) == 2:
+            step = min(count, HALF)
+            for at in range(0, count, step):
+                pieces.append((g, first + at, step, tile[:, :, at : at + step]))
+            if g == 0 and first + count == T:
                 offs_t = load_list(offs, "offs")
+        w1_raw = [sb([P, PACK, H], F32, "w1raw%d" % g) for g in range(2)]
         for g in range(2):
             nc.sync.dma_start(out=w1_raw[g][:], in_=w1[512 * g : 512 * (g + 1), :].rearrange("(p j) c -> p j c", j=PACK))
         pos_t = [load_list(src, "pos%d" % d) for d, src in enumerate((pos1, pos2, pos3, pos4))]
@@ -69,7 +76,7 @@ def tile_picked_sagecat_mean_e_kernel(tc, xT, w1, w2_words, w2_scales, w3_words,
         for name, words, scales in (("w3", w3_words, w3_scales), ("w2", w2_words, w2_scales)):
             wt = sb([P, 2 * N], U8, name + "_words")
             st = sb([P, N], U8, name + "_plane")
-            nc.gpsimd.memset(st[:], 0)
+            nc.gpsimd.memset(st[:].bitcast(I32), 0)
             nc.sync.dma_start(out=wt[:], in_=words[0])
             last_w.append((wt, st))
         for (wt, st), scales in zip(last_w, (w3_scales, w2_scales)):
@@ -79,18 +86,14 @@ def tile_picked_sagecat_mean_e_kernel(tc, xT, w1, w2_words, w2_scales, w3_words,
         ident = sb([P, P], F32, "ident")
         make_identity(nc, ident[:])
 
-        def flat(t):
-            return t[:].rearrange("p n j -> p (n j)")
-
         all_words = [sb([P, T], U32, "all_words%d" % g) for g in range(2)]
         all_bytes = sb([P, T], U8, "all_bytes")
-        nc.gpsimd.memset(all_bytes[:], 0)
+        nc.gpsimd.memset(all_bytes[:].bitcast(I32), 0)
 
-        for (g, first, count), tile in zip(chunks, raw):
+        for (g, first, count, raw), cut in zip(pieces, SCALAR_NODES):
             grouped = sb([P, count, PACK], BF16, "xg%d_%d" % (g, first))
-            cut = {(1, 0): 512, (1, 512): 384, (1, 1536): 160, (1, 1792): 160}.get((g, first), 256)
             dst = grouped[:].rearrange("p (c i) j -> p c j i", i=4)
-            src = tile.rearrange("p j (c i) -> p c j i", i=4)
+            src = raw.rearrange("p j (c i) -> p c j i", i=4)
             nc.scalar.activation(dst[:, 0 : cut // 4], src[:, 0 : cut // 4], ACT.Copy)
             if cut < count:
                 nc.vector.tensor_copy(dst[:, cut // 4 : count // 4], src[:, cut // 4 : count // 4])
@@ -100,102 +103,99 @@ def tile_picked_sagecat_mean_e_kernel(tc, xT, w1, w2_words, w2_scales, w3_words,
                 in_=flat(grouped),
             )
             if g == 0 and first + count == T:
-                early_words = sb([P, S], U32, "picked0")
-                nc.vector.tensor_copy(early_words[:], all_words[0][:].indirect(offs_t[:]))
+                words0 = sb([P, S], U32, "picked0")
+                nc.vector.tensor_copy(words0[:], all_words[0][:].indirect(offs_t[:]))
 
         picked_bytes = sb([P, S], U8, "picked_bytes")
         nc.vector.tensor_copy(picked_bytes[:], all_bytes[:].indirect(offs_t[:]))
-        def group_w1(dst, g, first, count):
+
+        def w1_views(dst, g, first, count):
             src = w1_raw[g][:].rearrange("p j (m t) -> p m j t", t=PACK)[:, :, :, first : first + count]
-            nc.scalar.copy(dst.rearrange("p t m j -> p m j t"), src)
+            return dst[:].rearrange("p t m j -> p m j t"), src
 
-        def w1_tile(passes, count, name, slot=None):
-            return sb([P, passes, count, P, PACK], BF16, name, slot)
-
-        def w1_flat(tile):
-            return tile[:].rearrange("p g t m j -> p (g t m j)")
+        def w1_flat(tile, first, count):
+            return tile[:, first : first + count].rearrange("p t m j -> p (t m j)")
 
         w1_q = {}
-        lead = [w1_tile(1, 1, "w1g_lead%d" % g) for g in range(2)]
-        second = w1_tile(2, 1, "w1g_second")
-        group_w1(lead[0][:, 0], 0, 0, 1)
-        codes, scales = quantise(w1_flat(lead[0]), "w1q_lead0")
-        w1_q[0, 0] = (codes[:], scales[:])
-        group_w1(second[:, 0], 0, 1, 1)
+
+        def quantise_w1(tile, g, first, count, slot=None):
+            codes, scales = quantise(w1_flat(tile, 0, count), "w1q%d_%d" % (g, first), slot)
+            for t in range(count):
+                w1_q[g, first + t] = (codes[:, P * t : P * (t + 1)], scales[:, P * t : P * (t + 1)])
+
         spans = ((0, 512), (512, 256), (768, 256))
-        late_words = {}
+        words1 = {}
 
-        def pick(first, count, tile, at):
-            nc.vector.tensor_copy(tile[:, at : at + count], all_words[1][:].indirect(entries(offs_t, first, count)))
-            late_words[first] = tile[:, at : at + count]
+        def pick(first, count, slot):
+            tile = sb([P, count], U32, "picked1_%d" % first, slot)
+            nc.vector.tensor_copy(tile[:], all_words[1][:].indirect(entries(offs_t, first, count)))
+            for start, width in spans:
+                if first <= start < first + count:
+                    words1[start] = tile[:, start - first : start - first + width]
 
-        pick(0, HALF, sb([P, HALF], U32, "picked10", "w1g_lead0"), 0)
-        src = w1_raw[1][:].rearrange("p j (m t) -> p m j t", t=PACK)[:, :, :, 0:1]
-        dst = lead[1][:, 0].rearrange("p t m j -> p m j t")
-        nc.scalar.copy(dst[:, 0:48], src[:, 0:48])
-        nc.vector.tensor_copy(dst[:, 48:P], src[:, 48:P])
-        codes, scales = quantise(w1_flat(lead[1]), "w1q_lead1")
-        w1_q[1, 0] = (codes[:], scales[:])
-        upper = sb([P, HALF], U32, "picked11", "w1g_lead1")
-        pick(512, 256, upper, 0)
-        pick(768, 256, upper, 256)
+        lead0 = sb([P, 2, P, PACK], BF16, "w1g_lead0")
+        nc.scalar.copy(*w1_views(lead0, 0, 0, 2))
+        quantise_w1(lead0, 0, 0, 2)
+        pick(0, 768, "w1g_lead0")
+        rest0 = sb([P, 2, P, PACK], BF16, "w1g_rest0")
+        nc.scalar.copy(*w1_views(rest0, 0, 2, 2))
+        lead1 = sb([P, 1, P, PACK], BF16, "w1g_lead1")
+        nc.scalar.copy(*w1_views(lead1, 1, 0, 1))
+        quantise_w1(lead1, 1, 0, 1)
+        pick(768, 256, "w1g_lead1")
 
         h = [sb([P, S], F32, "h%d" % t) for t in range(PACK)]
+        h_banks = {0: ("acc0", "acc1", "acc2"), 1: ("acc3", "acc1", "acc2"), 2: ("acc0", "back0", "back1"), 3: ("acc3", "acc1", "acc2")}
 
-        def hidden(t):
-            cuts = spans if t == 0 else ((0, HALF), (HALF, HALF))
-            names = ("acc%d0" % (t % 2), "acc%d1" % (t % 2), "sum0")
-            banks = [psum.tile([P, count], F32, name=name) for (first, count), name in zip(cuts, names)]
-            for g in range(2):
-                for (first, count), bank in zip(cuts, banks):
-                    if g == 0:
-                        words = early_words[:, first : first + count]
-                    elif first == 0:
-                        words = late_words[0]
-                    else:
-                        words = upper[:, first - HALF : first - HALF + count]
-                    nc.tensor.matmul_mx(
-                        out=bank[:],
-                        lhsT=w1_q[g, t][0].bitcast(FP8X4),
-                        lhsT_scale=w1_q[g, t][1],
-                        rhs=words.bitcast(FP8X4),
-                        rhs_scale=picked_bytes[4 * g : P, first : first + count],
-                        start=(g == 0),
-                        stop=(g == 1),
-                    )
-            for (first, count), bank in zip(cuts, banks):
-                if t == 0 and first > 0:
-                    nc.vector.tensor_scalar_max(h[t][:, first : first + count], bank[:], 0.0)
+        def product(t, g, banks):
+            for (first, count), acc in zip(spans, banks):
+                words = words0[:, first : first + count] if g == 0 else words1[first]
+                nc.tensor.matmul_mx(
+                    out=acc[:],
+                    lhsT=w1_q[g, t][0].bitcast(FP8X4),
+                    lhsT_scale=w1_q[g, t][1],
+                    rhs=words.bitcast(FP8X4),
+                    rhs_scale=picked_bytes[4 * g : P, first : first + count],
+                    start=(g == 0),
+                    stop=(g == 1),
+                )
+
+        def open_hidden(t):
+            banks = [bank([P, count], slot) for (first, count), slot in zip(spans, h_banks[t])]
+            product(t, 0, banks)
+            return banks
+
+        def close_hidden(t, banks):
+            product(t, 1, banks)
+            for (first, count), acc in zip(spans, banks):
+                if t == 0 and first == spans[2][0]:
+                    nc.vector.tensor_scalar_max(h[t][:, first : first + count], acc[:], 0.0)
                 else:
-                    nc.scalar.activation(h[t][:, first : first + count], bank[:], ACT.Relu)
+                    nc.scalar.activation(h[t][:, first : first + count], acc[:], ACT.Relu)
 
-        hidden(0)
-        group_w1(second[:, 1], 1, 1, 1)
-        codes, scales = quantise(w1_flat(second), "w1q_second")
-        for g in range(2):
-            w1_q[g, 1] = (codes[:, P * g : P * (g + 1)], scales[:, P * g : P * (g + 1)])
-        rest = w1_tile(2, 2, "w1g_rest")
-        for g in range(2):
-            group_w1(rest[:, g], g, 2, 2)
-        codes, scales = quantise(w1_flat(rest), "w1q_rest")
-        for g in range(2):
-            for t in (2, 3):
-                col = P * (2 * g + t - 2)
-                w1_q[g, t] = (codes[:, col : col + P], scales[:, col : col + P])
-        hidden(1)
-        hidden(2)
-        hidden(3)
+        banks0 = open_hidden(0)
+        close_hidden(0, banks0)
+        banks1 = open_hidden(1)
+        second1 = sb([P, 1, P, PACK], BF16, "w1g_second1")
+        nc.scalar.copy(*w1_views(second1, 1, 1, 1))
+        quantise_w1(second1, 1, 1, 1)
+        quantise_w1(rest0, 0, 2, 2, "w1q1_0_scales")
+        rest1 = sb([P, 2, P, PACK], BF16, "w1g_rest1", "w1q1_0_codes")
+        nc.scalar.copy(*w1_views(rest1, 1, 2, 2))
+        close_hidden(1, banks1)
+        quantise_w1(rest1, 1, 2, 2)
+        for t in (2, 3):
+            close_hidden(t, open_hidden(t))
 
-        pieces = ((0, 2), (2, 1), (3, 1))
         z_low = sb([P, 4, P, 2], BF16, "z_low")
-        z_high = {first: sb([P, blocks, P, 2], BF16, "z_high%d" % first) for first, blocks in pieces}
-        back = [psum.tile([P, 2, 256], F32, name="back%d" % vh) for vh in range(2)]
+        z_high = [sb([P, 2, P, 2], BF16, "z_high%d" % vh) for vh in range(2)]
+        back = [bank([P, 2, 256], "back%d" % vh) for vh in range(2)]
 
-        def add_neighbours(t, first, blocks, bank, slots):
-            total = psum.tile([P, blocks, P], F32, name=bank)
+        def add_neighbours(t, first, blocks, slot, last=None):
+            total = bank([P, blocks, P], slot)
             for d in range(4):
-                if d in slots:
-                    got = sb([P, P * blocks], F32, slots[d])
+                if d == 3 and last:
+                    got = sb([P, P * blocks], F32, last)
                 else:
                     got = ring.tile([P, P * blocks], F32, name="got")
                 nc.vector.tensor_copy(got[:], h[t][:].indirect(entries(pos_t[d], P * first, P * blocks)))
@@ -215,43 +215,52 @@ def tile_picked_sagecat_mean_e_kernel(tc, xT, w1, w2_words, w2_scales, w3_words,
                 c = first + b
                 nc.tensor.transpose(back[c // 2][:, u, P * (c % 2) : P * (c % 2 + 1)], words[:, P * b : P * (b + 1)], ident[:])
 
-        def group_z(first, blocks):
-            tile = sb([P, P * blocks * PACK], BF16, "zg%d" % first)
-            src = back[first // 2][:, :, P * (first % 2) : P * (first % 2 + blocks)]
-            nc.scalar.copy(tile[:].bitcast(F32).rearrange("p (v u) -> p v u", u=2), src.rearrange("p u v -> p v u"))
+        def group_z(vh):
+            tile = sb([P, 256 * PACK], BF16, "zg%d" % vh)
+            nc.scalar.copy(tile[:].bitcast(F32).rearrange("p (v u) -> p v u", u=2), back[vh][:].rearrange("p u v -> p v u"))
             return tile
 
         for t in range(2):
-            mean(z_low, t, add_neighbours(t, 0, 4, "sum%d" % t, {})[:])
+            mean(z_low, t, add_neighbours(t, 0, 4, "sum%d" % t)[:])
         turn_back(z_low, 0, 0, 4)
-        total = add_neighbours(2, 0, 4, "sum0", {})
-        for first, blocks in pieces:
-            mean(z_high[first], 0, total[:, first : first + blocks, :])
+        total = add_neighbours(2, 0, 4, "sum0")
+        for vh in range(2):
+            mean(z_high[vh], 0, total[:, 2 * vh : 2 * vh + 2, :])
+        z_grouped = []
+        for vh in range(2):
+            total = add_neighbours(3, 2 * vh, 2, "sum%d" % (1 - vh), "got_last%d" % vh)
+            mean(z_high[vh], 1, total[:])
+            turn_back(z_high[vh], 1, 2 * vh, 2)
+            z_grouped.append(group_z(vh))
 
-        stage = sb([P, PACK, 3 * P], BF16, "c_stage")
-        for t in range(PACK):
-            nc.vector.tensor_copy(stage[:, t, :], h[t][:].indirect(entries(cen_t, 0, 3 * P)))
-        c_early = sb([P, 3 * P, PACK], BF16, "c_early")
-        nc.scalar.copy(c_early[:].rearrange("p (c i) j -> p c j i", i=4), stage[:].rearrange("p j (c i) -> p c j i", i=4))
-        c_q = [quantise(flat(c_early)[:, 0 : 2 * P * PACK], "cq0"), quantise(flat(c_early)[:, 2 * P * PACK : 3 * P * PACK], "cq2")]
+        def stage_centres(first, count, slot=None):
+            stage = sb([P, PACK, count], BF16, "c_stage%d" % first, slot)
+            for t in range(PACK):
+                nc.vector.tensor_copy(stage[:, t, :], h[t][:].indirect(entries(cen_t, first, count)))
+            return stage
 
-        z_grouped = {}
-        for k, (first, blocks) in enumerate(pieces):
-            total = add_neighbours(3, first, blocks, "sum%d" % ((k + 1) % 2), {1: "got_last"} if first == 3 else {})
-            mean(z_high[first], 1, total[:])
-            turn_back(z_high[first], 1, first, blocks)
-            z_grouped[first] = group_z(first, blocks)
-        z_q = [quantise(z_grouped[0][:], "zq0", "got_last"), quantise(z_grouped[2][:], "zq2")]
-        tail = sb([P, P, PACK], BF16, "c_tail", "zg2")
+        def weave(stage, first, count, slot=None):
+            tile = sb([P, count, PACK], BF16, "c_grouped%d" % first, slot)
+            nc.scalar.copy(tile[:].rearrange("p (c i) j -> p c j i", i=4), stage[:].rearrange("p j (c i) -> p c j i", i=4))
+            return tile
+
+        stage01 = stage_centres(0, 256, "got_last0")
+        z_q = [quantise(z_grouped[0][:], "zq0")]
+        stage2 = stage_centres(256, P, "got_last1")
+        c01 = weave(stage01, 0, 256, "z_high1")
+        c2 = weave(stage2, 256, P, "got_last0")
+        z_q.append(quantise(z_grouped[1][:], "zq1"))
+        c_q = [quantise(flat(c01), "cq0")]
+        c_q.append(quantise(flat(c2), "cq2"))
+        tail = sb([P, P, PACK], BF16, "c_tail", "got_last1")
         for t in range(PACK):
             nc.vector.tensor_copy(tail[:, :, t], h[t][:].indirect(entries(cen_t, 3 * P, P)))
-        z_q.append(quantise(z_grouped[3][:], "zq3"))
         c_q.append(quantise(flat(tail), "cq3"))
 
         def operand(pair, first):
             return pair[0][:, first : first + P].bitcast(FP8X4), pair[1][:, first : first + P]
 
-        z_ops = [operand(z_q[0], 0), operand(z_q[0], P), operand(z_q[1], 0), operand(z_q[2], 0)]
+        z_ops = [operand(z_q[c // 2], P * (c % 2)) for c in range(4)]
         c_ops = [operand(c_q[0], 0), operand(c_q[0], P), operand(c_q[1], 0), operand(c_q[2], 0)]
 
         def last_pass(dst, which, mh, ops):
@@ -266,20 +275,26 @@ def tile_picked_sagecat_mean_e_kernel(tc, xT, w1, w2_words, w2_scales, w3_words,
                 stop=(which == 1),
             )
 
-        early = [psum.tile([P, 3 * P], F32, name="acc0%d" % mh) for mh in range(2)]
-        late = [psum.tile([P, P], F32, name="acc1%d" % mh) for mh in range(2)]
-        for c in range(3):
-            for mh in range(2):
+        out_v = out.rearrange("(a p) v -> p a v", p=P)
+        early = [bank([P, 2 * P], "acc%d" % mh) for mh in range(2)]
+        middle = [bank([P, P], "acc%d" % (2 + mh)) for mh in range(2)]
+        late = [bank([P, P], "sum%d" % mh) for mh in range(2)]
+        for mh in range(2):
+            for c in range(2):
                 last_pass(early[mh][:, P * c : P * (c + 1)], 0, mh, z_ops[c])
                 last_pass(early[mh][:, P * c : P * (c + 1)], 1, mh, c_ops[c])
         for mh in range(2):
+            last_pass(middle[mh][:], 0, mh, z_ops[2])
             last_pass(late[mh][:], 0, mh, z_ops[3])
-        for mh in range(2):
-            last_pass(late[mh][:], 1, mh, c_ops[3])
-        out_v = out.rearrange("(a p) v -> p a v", p=P)
         res_early = sb([P, 2, 3 * P], F32, "res_early")
         for mh in range(2):
-            nc.scalar.copy(res_early[:, mh, :], early[mh][:])
+            nc.scalar.copy(res_early[:, mh, 0 : 2 * P], early[mh][:])
+        for mh in range(2):
+            last_pass(middle[mh][:], 1, mh, c_ops[2])
+        for mh in range(2):
+            last_pass(late[mh][:], 1, mh, c_ops[3])
+        for mh in range(2):
+            nc.scalar.copy(res_early[:, mh, 2 * P : 3 * P], middle[mh][:])
         nc.sync.dma_start(out=out_v[:, :, 0 : 3 * P], in_=res_early[:])
         res_late = sb([P, 2, P], F32, "res_late")
         nc.scalar.copy(res_late[:, 0, :], late[0][:])

@@ -21,7 +21,7 @@ PACK = 4
 HALF = 512
 
 LOADS = ((0, 0, 1024), (0, 1024, 1024), (1, 0, 512), (1, 512, 512), (1, 1024, 512), (1, 1536, 256), (1, 1792, 256))
-SCALAR_NODES = (320, 320, 256, 256, 512, 384, 320, 144, 128)
+SCALAR_NODES = (320, 320, 256, 256, 512, 384, 320, 128, 96)
 
 
 def tile_picked_sagecat_mean_e_kernel(tc, xT, w1, w2_words, w2_scales, w3_words, w3_scales, offs, cen, pos1, pos2, pos3, pos4, out):
@@ -29,7 +29,6 @@ def tile_picked_sagecat_mean_e_kernel(tc, xT, w1, w2_words, w2_scales, w3_words,
     with ExitStack() as ctx:
         lists = ctx.enter_context(tc.tile_pool(name="lists", bufs=1))
         keep = ctx.enter_context(tc.tile_pool(name="keep", bufs=1))
-        ring = ctx.enter_context(tc.tile_pool(name="ring", bufs=8))
         psum = ctx.enter_context(tc.psum_pool(name="psum", bufs=1))
 
         def sb(shape, dtype, name, slot=None):
@@ -191,14 +190,13 @@ def tile_picked_sagecat_mean_e_kernel(tc, xT, w1, w2_words, w2_scales, w3_words,
         z_high = [sb([P, 2, P, 2], BF16, "z_high%d" % vh) for vh in range(2)]
         back = [bank([P, 2, 256], "back%d" % vh) for vh in range(2)]
 
-        def add_neighbours(t, first, blocks, slot, last=None):
+        def add_neighbours(t, first, blocks, slot):
             total = bank([P, blocks, P], slot)
+            name = "got%d_%d" % (t, first)
+            halves = [sb([P, 2, P * blocks], F32, name + "_low"), sb([P, 2, P * blocks], F32, name + "_high", "w1raw1" if t == 0 else None)]
             for d in range(4):
-                if d == 3 and last:
-                    got = sb([P, P * blocks], F32, last)
-                else:
-                    got = ring.tile([P, P * blocks], F32, name="got")
-                nc.vector.tensor_copy(got[:], h[t][:].indirect(entries(pos_t[d], P * first, P * blocks)))
+                got = halves[d // 2][:, d % 2]
+                nc.vector.tensor_copy(got, h[t][:].indirect(entries(pos_t[d], P * first, P * blocks)))
                 for b in range(blocks):
                     nc.tensor.matmul(
                         total[:, b, :], got[:, P * b : P * (b + 1)], ident[:],
@@ -228,7 +226,7 @@ def tile_picked_sagecat_mean_e_kernel(tc, xT, w1, w2_words, w2_scales, w3_words,
             mean(z_high[vh], 0, total[:, 2 * vh : 2 * vh + 2, :])
         z_grouped = []
         for vh in range(2):
-            total = add_neighbours(3, 2 * vh, 2, "sum%d" % (1 - vh), "got_last%d" % vh)
+            total = add_neighbours(3, 2 * vh, 2, "sum%d" % (1 - vh))
             mean(z_high[vh], 1, total[:])
             turn_back(z_high[vh], 1, 2 * vh, 2)
             z_grouped.append(group_z(vh))
@@ -244,15 +242,15 @@ def tile_picked_sagecat_mean_e_kernel(tc, xT, w1, w2_words, w2_scales, w3_words,
             nc.scalar.copy(tile[:].rearrange("p (c i) j -> p c j i", i=4), stage[:].rearrange("p j (c i) -> p c j i", i=4))
             return tile
 
-        stage01 = stage_centres(0, 256, "got_last0")
+        stage01 = stage_centres(0, 256, "got3_0_high")
         z_q = [quantise(z_grouped[0][:], "zq0")]
-        stage2 = stage_centres(256, P, "got_last1")
+        stage2 = stage_centres(256, P, "got3_2_high")
         c01 = weave(stage01, 0, 256, "z_high1")
-        c2 = weave(stage2, 256, P, "got_last0")
+        c2 = weave(stage2, 256, P, "got3_0_high")
         z_q.append(quantise(z_grouped[1][:], "zq1"))
         c_q = [quantise(flat(c01), "cq0")]
         c_q.append(quantise(flat(c2), "cq2"))
-        tail = sb([P, P, PACK], BF16, "c_tail", "got_last1")
+        tail = sb([P, P, PACK], BF16, "c_tail", "got3_2_high")
         for t in range(PACK):
             nc.vector.tensor_copy(tail[:, :, t], h[t][:].indirect(entries(cen_t, 3 * P, P)))
         c_q.append(quantise(flat(tail), "cq3"))

@@ -20,8 +20,8 @@ P = 128
 PACK = 4
 HALF = 512
 
-LOADS = ((0, 0, 1024), (0, 1024, 1024), (1, 0, 512), (1, 512, 512), (1, 1024, 512), (1, 1536, 256), (1, 1792, 256))
-SCALAR_NODES = (320, 320, 256, 256, 512, 384, 320, 128, 96)
+LOADS = ((0, 0, 1024), (0, 1024, 512), (0, 1536, 512), (1, 0, 512), (1, 512, 512), (1, 1024, 512), (1, 1536, 256), (1, 1792, 256))
+SCALAR_NODES = (320, 320, 320, 256, 512, 320, 288, 128, 96)
 
 
 def tile_picked_sagecat_mean_e_kernel(tc, xT, w1, w2_words, w2_scales, w3_words, w3_scales, offs, cen, pos1, pos2, pos3, pos4, out):
@@ -144,7 +144,7 @@ def tile_picked_sagecat_mean_e_kernel(tc, xT, w1, w2_words, w2_scales, w3_words,
         pick(768, 256, "w1g_lead1")
 
         h = [sb([P, S], F32, "h%d" % t) for t in range(PACK)]
-        h_banks = {0: ("acc0", "acc1", "acc2"), 1: ("acc3", "acc1", "acc2"), 2: ("acc0", "back0", "back1"), 3: ("acc3", "acc1", "acc2")}
+        h_banks = {0: ("acc0", "acc1", "acc2"), 1: ("acc3", "back0", "back1"), 2: ("acc0", "acc1", "acc2"), 3: ("acc3", "back0", "back1")}
 
         def product(t, g, banks):
             for (first, count), acc in zip(spans, banks):
@@ -167,7 +167,7 @@ def tile_picked_sagecat_mean_e_kernel(tc, xT, w1, w2_words, w2_scales, w3_words,
         def close_hidden(t, banks):
             product(t, 1, banks)
             for (first, count), acc in zip(spans, banks):
-                if t == 0 and first == spans[2][0]:
+                if t == 0 and first == spans[1][0]:
                     nc.vector.tensor_scalar_max(h[t][:, first : first + count], acc[:], 0.0)
                 else:
                     nc.scalar.activation(h[t][:, first : first + count], acc[:], ACT.Relu)

@@ -20,8 +20,12 @@ P = 128
 PACK = 4
 HALF = 512
 
-LOADS = ((0, 0, 1024), (0, 1024, 512), (0, 1536, 512), (1, 0, 512), (1, 512, 512), (1, 1024, 512), (1, 1536, 256), (1, 1792, 256))
-SCALAR_NODES = (320, 320, 320, 256, 512, 320, 288, 128, 96)
+LOADS = (
+    (0, 0, 2048, 704),
+    (1, 0, 1024, 1024), (1, 1024, 1024, 352),
+    (2, 0, 1024, 1024), (2, 1024, 1024, 0),
+    (3, 0, 1024, 1024), (3, 1024, 512, 0), (3, 1536, 256, 256), (3, 1792, 256, 96),
+)
 
 
 def tile_picked_sagecat_mean_e_kernel(tc, xT, w1, w2_words, w2_scales, w3_words, w3_scales, offs, cen, pos1, pos2, pos3, pos4, out):
@@ -55,15 +59,14 @@ def tile_picked_sagecat_mean_e_kernel(tc, xT, w1, w2_words, w2_scales, w3_words,
             nc.sync.dma_start(tile[:], src)
             return tile
 
-        pieces = []
-        for g, first, count in LOADS:
-            tile = sb([P, PACK, count], F32, "x%d_%d" % (g, first))
+        raw = []
+        for pair, first, count, cut in LOADS:
+            g, u = divmod(pair, 2)
+            tile = sb([P, 2, count], F32, "x%d_%d" % (pair, first))
             rows = xT[512 * g : 512 * (g + 1), :].rearrange("(p j) t -> p j t", j=PACK)
-            nc.sync.dma_start(out=tile[:], in_=rows[:, :, first : first + count])
-            step = min(count, HALF)
-            for at in range(0, count, step):
-                pieces.append((g, first + at, step, tile[:, :, at : at + step]))
-            if g == 0 and first + count == T:
+            nc.sync.dma_start(out=tile[:], in_=rows[:, 2 * u : 2 * u + 2, first : first + count])
+            raw.append(tile)
+            if pair == 0:
                 offs_t = load_list(offs, "offs")
         w1_raw = [sb([P, PACK, H], F32, "w1raw%d" % g) for g in range(2)]
         for g in range(2):
@@ -85,28 +88,52 @@ def tile_picked_sagecat_mean_e_kernel(tc, xT, w1, w2_words, w2_scales, w3_words,
         ident = sb([P, P], F32, "ident")
         make_identity(nc, ident[:])
 
-        all_words = [sb([P, T], U32, "all_words%d" % g) for g in range(2)]
-        all_bytes = sb([P, T], U8, "all_bytes")
-        nc.gpsimd.memset(all_bytes[:].bitcast(I32), 0)
+        spans = ((0, 512), (512, 256), (768, 256))
+        pairs = [sb([P, T, 2], BF16, "pairs%d" % pair) for pair in range(4)]
+        got_pairs = [sb([P, 2, S], U32, "got_pairs%d" % g) for g in range(2)]
+        picked = {}
 
-        for (g, first, count, raw), cut in zip(pieces, SCALAR_NODES):
-            grouped = sb([P, count, PACK], BF16, "xg%d_%d" % (g, first))
-            dst = grouped[:].rearrange("p (c i) j -> p c j i", i=4)
-            src = raw.rearrange("p j (c i) -> p c j i", i=4)
-            nc.scalar.activation(dst[:, 0 : cut // 4], src[:, 0 : cut // 4], ACT.Copy)
+        def pick(pair, first, count):
+            g, u = divmod(pair, 2)
+            window = pairs[pair][:].rearrange("p n e -> p (n e)").bitcast(U32)
+            nc.vector.tensor_copy(got_pairs[g][:, u, first : first + count], window.indirect(entries(offs_t, first, count)))
+
+        def weave_pairs(g, first, count, on_scalar, tile):
+            dst = tile.rearrange("p (c i) u -> p c u i", i=4)
+            src = got_pairs[g][:, :, first : first + count].rearrange("p u (c i) -> p c u i", i=4)
+            if on_scalar:
+                nc.scalar.copy(dst, src)
+            else:
+                nc.vector.tensor_copy(dst.bitcast(I32), src.bitcast(I32))
+            picked[g, first] = tile.rearrange("p n u -> p (n u)").bitcast(BF16)
+
+        x_q = {}
+
+        def quantise_x(g, first, count, slot=None):
+            codes, scales = quantise(picked[g, first], "xq%d_%d" % (g, first), slot)
+            for start, width in spans:
+                if first <= start < first + count:
+                    at = start - first
+                    x_q[g, start] = (codes[:, at : at + width], scales[:, at : at + width])
+
+        for (pair, first, count, cut), tile in zip(LOADS, raw):
+            dst = pairs[pair][:, first : first + count].rearrange("p (c i) e -> p c e i", i=4)
+            src = tile[:].rearrange("p e (c i) -> p c e i", i=4)
+            if cut > 0:
+                nc.scalar.activation(dst[:, 0 : cut // 4], src[:, 0 : cut // 4], ACT.Copy)
             if cut < count:
                 nc.vector.tensor_copy(dst[:, cut // 4 : count // 4], src[:, cut // 4 : count // 4])
-            nc.vector.quantize_mx(
-                out=all_words[g][:, first : first + count].bitcast(FP8X4),
-                scales=all_bytes[4 * g : P, first : first + count],
-                in_=flat(grouped),
-            )
-            if g == 0 and first + count == T:
-                words0 = sb([P, S], U32, "picked0")
-                nc.vector.tensor_copy(words0[:], all_words[0][:].indirect(offs_t[:]))
-
-        picked_bytes = sb([P, S], U8, "picked_bytes")
-        nc.vector.tensor_copy(picked_bytes[:], all_bytes[:].indirect(offs_t[:]))
+            if first + count == T and pair % 2 == 0:
+                pick(pair, 0, S)
+            if first + count == T and pair % 2 == 1:
+                pick(pair, 0, HALF)
+                pick(pair, HALF, HALF)
+            if first + count == T and pair == 1:
+                weave_pairs(0, 0, HALF, False, sb([P, HALF, 2], U32, "picked0_low")[:])
+                quantise_x(0, 0, HALF)
+            if pair == 2 and first == 0:
+                weave_pairs(0, HALF, HALF, True, sb([P, HALF, 2], U32, "picked0_high", "x2_0")[:])
+                quantise_x(0, HALF, HALF)
 
         def w1_views(dst, g, first, count):
             src = w1_raw[g][:].rearrange("p j (m t) -> p m j t", t=PACK)[:, :, :, first : first + count]
@@ -122,39 +149,31 @@ def tile_picked_sagecat_mean_e_kernel(tc, xT, w1, w2_words, w2_scales, w3_words,
             for t in range(count):
                 w1_q[g, first + t] = (codes[:, P * t : P * (t + 1)], scales[:, P * t : P * (t + 1)])
 
-        spans = ((0, 512), (512, 256), (768, 256))
-        words1 = {}
-
-        def pick(first, count, slot):
-            tile = sb([P, count], U32, "picked1_%d" % first, slot)
-            nc.vector.tensor_copy(tile[:], all_words[1][:].indirect(entries(offs_t, first, count)))
-            for start, width in spans:
-                if first <= start < first + count:
-                    words1[start] = tile[:, start - first : start - first + width]
-
         lead0 = sb([P, 2, P, PACK], BF16, "w1g_lead0")
         nc.scalar.copy(*w1_views(lead0, 0, 0, 2))
         quantise_w1(lead0, 0, 0, 2)
-        pick(0, 768, "w1g_lead0")
+        picked1 = sb([P, S, 2], U32, "picked1", "w1g_lead0")
+        for first in (0, HALF):
+            weave_pairs(1, first, HALF, False, picked1[:, first : first + HALF])
+        quantise_x(1, 0, HALF)
         rest0 = sb([P, 2, P, PACK], BF16, "w1g_rest0")
         nc.scalar.copy(*w1_views(rest0, 0, 2, 2))
         lead1 = sb([P, 1, P, PACK], BF16, "w1g_lead1")
         nc.scalar.copy(*w1_views(lead1, 1, 0, 1))
         quantise_w1(lead1, 1, 0, 1)
-        pick(768, 256, "w1g_lead1")
+        quantise_x(1, HALF, HALF, "w1g_lead1")
 
         h = [sb([P, S], F32, "h%d" % t) for t in range(PACK)]
         h_banks = {0: ("acc0", "acc1", "acc2"), 1: ("acc3", "back0", "back1"), 2: ("acc0", "acc1", "acc2"), 3: ("acc3", "back0", "back1")}
 
         def product(t, g, banks):
             for (first, count), acc in zip(spans, banks):
-                words = words0[:, first : first + count] if g == 0 else words1[first]
                 nc.tensor.matmul_mx(
                     out=acc[:],
                     lhsT=w1_q[g, t][0].bitcast(FP8X4),
                     lhsT_scale=w1_q[g, t][1],
-                    rhs=words.bitcast(FP8X4),
-                    rhs_scale=picked_bytes[4 * g : P, first : first + count],
+                    rhs=x_q[g, first][0].bitcast(FP8X4),
+                    rhs_scale=x_q[g, first][1],
                     start=(g == 0),
                     stop=(g == 1),
                 )
@@ -178,7 +197,7 @@ def tile_picked_sagecat_mean_e_kernel(tc, xT, w1, w2_words, w2_scales, w3_words,
         second1 = sb([P, 1, P, PACK], BF16, "w1g_second1")
         nc.scalar.copy(*w1_views(second1, 1, 1, 1))
         quantise_w1(second1, 1, 1, 1)
-        quantise_w1(rest0, 0, 2, 2, "w1q1_0_scales")
+        quantise_w1(rest0, 0, 2, 2, "w1g_second1")
         rest1 = sb([P, 2, P, PACK], BF16, "w1g_rest1", "w1q1_0_codes")
         nc.scalar.copy(*w1_views(rest1, 1, 2, 2))
         close_hidden(1, banks1)

@@ -23,7 +23,7 @@ HALF = 512
 LOADS = (
     (0, 0, 2048, 704),
     (1, 0, 1024, 1024), (1, 1024, 1024, 352),
-    (2, 0, 1024, 1024), (2, 1024, 1024, 0),
+    (2, 0, 1024, 1024), (2, 1024, 1024, 256),
     (3, 0, 1024, 1024), (3, 1024, 512, 0), (3, 1536, 256, 256), (3, 1792, 256, 96),
 )
 
@@ -161,7 +161,7 @@ def tile_picked_sagecat_mean_e_kernel(tc, xT, w1, w2_words, w2_scales, w3_words,
         lead1 = sb([P, 1, P, PACK], BF16, "w1g_lead1")
         nc.scalar.copy(*w1_views(lead1, 1, 0, 1))
         quantise_w1(lead1, 1, 0, 1)
-        quantise_x(1, HALF, HALF, "w1g_lead1")
+        quantise_x(1, HALF, HALF)
 
         h = [sb([P, S], F32, "h%d" % t) for t in range(PACK)]
         h_banks = {0: ("acc0", "acc1", "acc2"), 1: ("acc3", "back0", "back1"), 2: ("acc0", "acc1", "acc2"), 3: ("acc3", "back0", "back1")}
@@ -197,7 +197,7 @@ def tile_picked_sagecat_mean_e_kernel(tc, xT, w1, w2_words, w2_scales, w3_words,
         second1 = sb([P, 1, P, PACK], BF16, "w1g_second1")
         nc.scalar.copy(*w1_views(second1, 1, 1, 1))
         quantise_w1(second1, 1, 1, 1)
-        quantise_w1(rest0, 0, 2, 2, "w1g_second1")
+        quantise_w1(rest0, 0, 2, 2, "w1g_lead1")
         rest1 = sb([P, 2, P, PACK], BF16, "w1g_rest1", "w1q1_0_codes")
         nc.scalar.copy(*w1_views(rest1, 1, 2, 2))
         close_hidden(1, banks1)

@@ -23,8 +23,8 @@ HALF = 512
 LOADS = (
     (0, 0, 2048, 704),
     (1, 0, 1024, 1024), (1, 1024, 1024, 352),
-    (2, 0, 1024, 1024), (2, 1024, 1024, 256),
-    (3, 0, 1024, 1024), (3, 1024, 512, 0), (3, 1536, 256, 256), (3, 1792, 256, 96),
+    (2, 0, 1024, 1024), (2, 1024, 1024, 0),
+    (3, 0, 1024, 1024), (3, 1024, 512, 0), (3, 1536, 256, 128), (3, 1792, 256, 96),
 )
 
 

@@ -32,11 +32,15 @@ def tile_picked_sagecat_mean_e_kernel(tc, xT, w1, w2_words, w2_scales, w3_words,
     nc = tc.nc
     with ExitStack() as ctx:
         lists = ctx.enter_context(tc.tile_pool(name="lists", bufs=1))
+        hidden = ctx.enter_context(tc.tile_pool(name="hidden", bufs=1))
         keep = ctx.enter_context(tc.tile_pool(name="keep", bufs=1))
+        fetched = ctx.enter_context(tc.tile_pool(name="fetched", bufs=1))
         psum = ctx.enter_context(tc.psum_pool(name="psum", bufs=1))
 
         def sb(shape, dtype, name, slot=None):
-            return keep.tile(shape, dtype, name=name, tag=slot or name, align_bytes=64)
+            tag = slot or name
+            pool = fetched if tag.startswith("got") or tag.startswith("c_") else keep
+            return pool.tile(shape, dtype, name=name, tag=tag, align_bytes=64)
 
         def bank(shape, slot):
             return psum.tile(shape, F32, name=slot)
@@ -163,7 +167,7 @@ def tile_picked_sagecat_mean_e_kernel(tc, xT, w1, w2_words, w2_scales, w3_words,
         quantise_w1(lead1, 1, 0, 1)
         quantise_x(1, HALF, HALF)
 
-        h = [sb([P, S], F32, "h%d" % t) for t in range(PACK)]
+        h = [hidden.tile([P, S], F32, name="h%d" % t, align_bytes=64) for t in range(PACK)]
         h_banks = {0: ("acc0", "acc1", "acc2"), 1: ("acc3", "back0", "back1"), 2: ("acc0", "acc1", "acc2"), 3: ("acc3", "back0", "back1")}
 
         def product(t, g, banks):

@@ -20,36 +20,31 @@ P = 128
 PACK = 4
 HALF = 512
 
-LOADS = (
-    (0, 0, 2048, 704),
-    (1, 0, 1024, 1024), (1, 1024, 1024, 352),
-    (2, 0, 1024, 1024), (2, 1024, 1024, 0),
-    (3, 0, 1024, 1024), (3, 1024, 512, 0), (3, 1536, 256, 128), (3, 1792, 256, 96),
-)
+VECTOR_ENTRIES = (0, 1024, 0, 768, 0, 512, 256, 256)
+VECTOR_LISTS = (4, 2, 2, 1)
 
 
 def tile_picked_sagecat_mean_e_kernel(tc, xT, w1, w2_words, w2_scales, w3_words, w3_scales, offs, cen, pos1, pos2, pos3, pos4, out):
     nc = tc.nc
     with ExitStack() as ctx:
         lists = ctx.enter_context(tc.tile_pool(name="lists", bufs=1))
-        hidden = ctx.enter_context(tc.tile_pool(name="hidden", bufs=1))
         keep = ctx.enter_context(tc.tile_pool(name="keep", bufs=1))
-        fetched = ctx.enter_context(tc.tile_pool(name="fetched", bufs=1))
         psum = ctx.enter_context(tc.psum_pool(name="psum", bufs=1))
 
         def sb(shape, dtype, name, slot=None):
-            tag = slot or name
-            pool = fetched if tag.startswith("got") or tag.startswith("c_") else keep
-            return pool.tile(shape, dtype, name=name, tag=tag, align_bytes=64)
+            return keep.tile(shape, dtype, name=name, tag=slot or name, align_bytes=64)
 
         def bank(shape, slot):
-            return psum.tile(shape, F32, name=slot)
+            return psum.tile(shape, F32, name="bank%d" % slot)
 
         def entries(tile, first, count):
             return tile[:, first // 16 : (first + count) // 16]
 
-        def flat(tile):
-            return tile[:].rearrange("p n j -> p (n j)")
+        def gather(on_vector, dst, window, offsets):
+            if on_vector:
+                nc.vector.tensor_copy(dst, window.indirect(offsets))
+            else:
+                nc.scalar.activation(dst, window.indirect(offsets), ACT.Copy)
 
         def quantise(grouped, name, slot=None):
             width = grouped.shape[1] // PACK
@@ -58,19 +53,30 @@ def tile_picked_sagecat_mean_e_kernel(tc, xT, w1, w2_words, w2_scales, w3_words,
             nc.vector.quantize_mx(out=codes[:].bitcast(FP8X4), scales=scales[:], in_=grouped)
             return codes, scales
 
+        def weave(grouped, planes, first, count, on_vector=True):
+            dst = grouped.rearrange("p (c i) j -> p c j i", i=4)[:, :, first : first + count]
+            src = planes.rearrange("p j (c i) -> p c j i", i=4)[:, :, first : first + count]
+            if on_vector:
+                nc.vector.tensor_copy(dst, src)
+            else:
+                nc.scalar.activation(dst, src, ACT.Copy)
+
+        def flat(tile):
+            return tile[:].rearrange("p n j -> p (n j)")
+
         def load_list(src, name):
             tile = lists.tile([P, src.shape[1]], U16, name=name)
             nc.sync.dma_start(tile[:], src)
             return tile
 
-        raw = []
-        for pair, first, count, cut in LOADS:
-            g, u = divmod(pair, 2)
-            tile = sb([P, 2, count], F32, "x%d_%d" % (pair, first))
+        x_raw = []
+        for plane in range(2 * PACK):
+            g, j = divmod(plane, PACK)
+            tile = sb([P, T], F32, "x%d" % plane)
             rows = xT[512 * g : 512 * (g + 1), :].rearrange("(p j) t -> p j t", j=PACK)
-            nc.sync.dma_start(out=tile[:], in_=rows[:, 2 * u : 2 * u + 2, first : first + count])
-            raw.append(tile)
-            if pair == 0:
+            nc.sync.dma_start(out=tile[:], in_=rows[:, j, :])
+            x_raw.append(tile)
+            if plane == 0:
                 offs_t = load_list(offs, "offs")
         w1_raw = [sb([P, PACK, H], F32, "w1raw%d" % g) for g in range(2)]
         for g in range(2):
@@ -79,7 +85,7 @@ def tile_picked_sagecat_mean_e_kernel(tc, xT, w1, w2_words, w2_scales, w3_words,
         cen_t = load_list(cen, "cen")
 
         last_w = []
-        for name, words, scales in (("w3", w3_words, w3_scales), ("w2", w2_words, w2_scales)):
+        for name, words in (("w3", w3_words), ("w2", w2_words)):
             wt = sb([P, 2 * N], U8, name + "_words")
             st = sb([P, N], U8, name + "_plane")
             nc.gpsimd.memset(st[:].bitcast(I32), 0)
@@ -92,232 +98,177 @@ def tile_picked_sagecat_mean_e_kernel(tc, xT, w1, w2_words, w2_scales, w3_words,
         ident = sb([P, P], F32, "ident")
         make_identity(nc, ident[:])
 
-        spans = ((0, 512), (512, 256), (768, 256))
-        pairs = [sb([P, T, 2], BF16, "pairs%d" % pair) for pair in range(4)]
-        got_pairs = [sb([P, 2, S], U32, "got_pairs%d" % g) for g in range(2)]
-        picked = {}
-
-        def pick(pair, first, count):
-            g, u = divmod(pair, 2)
-            window = pairs[pair][:].rearrange("p n e -> p (n e)").bitcast(U32)
-            nc.vector.tensor_copy(got_pairs[g][:, u, first : first + count], window.indirect(entries(offs_t, first, count)))
-
-        def weave_pairs(g, first, count, on_scalar, tile):
-            dst = tile.rearrange("p (c i) u -> p c u i", i=4)
-            src = got_pairs[g][:, :, first : first + count].rearrange("p u (c i) -> p c u i", i=4)
-            if on_scalar:
-                nc.scalar.copy(dst, src)
-            else:
-                nc.vector.tensor_copy(dst.bitcast(I32), src.bitcast(I32))
-            picked[g, first] = tile.rearrange("p n u -> p (n u)").bitcast(BF16)
-
+        planes = [sb([P, PACK, S], BF16, "planes%d" % g) for g in range(2)]
+        x_grouped = [[sb([P, HALF, PACK], BF16, "xg%d_%d" % (g, half)) for half in range(2)] for g in range(2)]
         x_q = {}
 
-        def quantise_x(g, first, count, slot=None):
-            codes, scales = quantise(picked[g, first], "xq%d_%d" % (g, first), slot)
-            for start, width in spans:
-                if first <= start < first + count:
-                    at = start - first
-                    x_q[g, start] = (codes[:, at : at + width], scales[:, at : at + width])
+        def pick(plane, on_vector, first, count):
+            g, j = divmod(plane, PACK)
+            gather(on_vector, planes[g][:, j, first : first + count], x_raw[plane][:], entries(offs_t, first, count))
 
-        for (pair, first, count, cut), tile in zip(LOADS, raw):
-            dst = pairs[pair][:, first : first + count].rearrange("p (c i) e -> p c e i", i=4)
-            src = tile[:].rearrange("p e (c i) -> p c e i", i=4)
+        def weave_x(g, first, count, j_first, j_count, on_vector=True):
+            half, at = divmod(first, HALF)
+            weave(x_grouped[g][half][:, at : at + count], planes[g][:, :, first : first + count], j_first, j_count, on_vector)
+
+        for plane, cut in enumerate(VECTOR_ENTRIES):
+            last = plane == 2 * PACK - 1
             if cut > 0:
-                nc.scalar.activation(dst[:, 0 : cut // 4], src[:, 0 : cut // 4], ACT.Copy)
-            if cut < count:
-                nc.vector.tensor_copy(dst[:, cut // 4 : count // 4], src[:, cut // 4 : count // 4])
-            if first + count == T and pair % 2 == 0:
-                pick(pair, 0, S)
-            if first + count == T and pair % 2 == 1:
-                pick(pair, 0, HALF)
-                pick(pair, HALF, HALF)
-            if first + count == T and pair == 1:
-                weave_pairs(0, 0, HALF, False, sb([P, HALF, 2], U32, "picked0_low")[:])
-                quantise_x(0, 0, HALF)
-            if pair == 2 and first == 0:
-                weave_pairs(0, HALF, HALF, True, sb([P, HALF, 2], U32, "picked0_high", "x2_0")[:])
-                quantise_x(0, HALF, HALF)
-
-        def w1_views(dst, g, first, count):
-            src = w1_raw[g][:].rearrange("p j (m t) -> p m j t", t=PACK)[:, :, :, first : first + count]
-            return dst[:].rearrange("p t m j -> p m j t"), src
-
-        def w1_flat(tile, first, count):
-            return tile[:, first : first + count].rearrange("p t m j -> p (t m j)")
+                pick(plane, True, 0, cut)
+            if last:
+                for first in range(cut, S, 256):
+                    pick(plane, False, first, 256)
+            elif cut < S:
+                pick(plane, False, cut, S - cut)
+            if plane == 1:
+                weave_x(0, 0, HALF, 0, 2)
+                weave_x(0, HALF, HALF - P, 0, 2)
+            if plane == 3:
+                weave_x(0, 0, HALF, 2, 2)
+                weave_x(0, HALF, HALF - P, 2, 2)
+                weave_x(0, S - P, P, 0, PACK, False)
+                for half in range(2):
+                    x_q[0, half] = quantise(flat(x_grouped[0][half]), "xq0_%d" % half)
+            if plane == 5:
+                for half in range(2):
+                    weave_x(1, HALF * half, HALF, 0, 2)
+        for first in range(0, S, 256):
+            weave_x(1, first, 256, 2, 2)
 
         w1_q = {}
 
+        def deal_w1(g, cut):
+            tile = sb([P, PACK, P, PACK], BF16, "w1g%d" % g)
+            src = w1_raw[g][:].rearrange("p j (m t) -> p m j t", t=PACK)
+            dst = tile[:].rearrange("p t m j -> p m j t")
+            nc.scalar.activation(dst[:, cut:P], src[:, cut:P], ACT.Copy)
+            nc.vector.tensor_copy(dst[:, 0:cut], src[:, 0:cut])
+            return tile
+
         def quantise_w1(tile, g, first, count, slot=None):
-            codes, scales = quantise(w1_flat(tile, 0, count), "w1q%d_%d" % (g, first), slot)
-            for t in range(count):
-                w1_q[g, first + t] = (codes[:, P * t : P * (t + 1)], scales[:, P * t : P * (t + 1)])
+            codes, scales = quantise(tile[:, first : first + count].rearrange("p t m j -> p (t m j)"), "w1q%d_%d" % (g, first), slot)
+            for e in range(count):
+                w1_q[g, first + e] = (codes[:, P * e : P * (e + 1)], scales[:, P * e : P * (e + 1)])
 
-        lead0 = sb([P, 2, P, PACK], BF16, "w1g_lead0")
-        nc.scalar.copy(*w1_views(lead0, 0, 0, 2))
-        quantise_w1(lead0, 0, 0, 2)
-        picked1 = sb([P, S, 2], U32, "picked1", "w1g_lead0")
-        for first in (0, HALF):
-            weave_pairs(1, first, HALF, False, picked1[:, first : first + HALF])
-        quantise_x(1, 0, HALF)
-        rest0 = sb([P, 2, P, PACK], BF16, "w1g_rest0")
-        nc.scalar.copy(*w1_views(rest0, 0, 2, 2))
-        lead1 = sb([P, 1, P, PACK], BF16, "w1g_lead1")
-        nc.scalar.copy(*w1_views(lead1, 1, 0, 1))
-        quantise_w1(lead1, 1, 0, 1)
-        quantise_x(1, HALF, HALF)
+        x_q[1, 0] = quantise(flat(x_grouped[1][0]), "xq1_0")
+        dealt0 = deal_w1(0, 32)
+        x_q[1, 1] = quantise(flat(x_grouped[1][1]), "xq1_1")
+        quantise_w1(dealt0, 0, 0, 1)
+        dealt1 = deal_w1(1, 70)
+        quantise_w1(dealt1, 1, 0, 1)
+        quantise_w1(dealt0, 0, 1, 3, "w1raw1")
+        quantise_w1(dealt1, 1, 1, 3)
 
-        h = [hidden.tile([P, S], F32, name="h%d" % t, align_bytes=64) for t in range(PACK)]
-        h_banks = {0: ("acc0", "acc1", "acc2"), 1: ("acc3", "back0", "back1"), 2: ("acc0", "acc1", "acc2"), 3: ("acc3", "back0", "back1")}
+        h = [sb([P, S], F32, "h%d" % t) for t in range(PACK)]
+        h_banks = [[bank([P, HALF], 2 * t + half) for half in range(2)] for t in range(PACK)]
 
-        def product(t, g, banks):
-            for (first, count), acc in zip(spans, banks):
+        def product(t, g):
+            for half in range(2):
                 nc.tensor.matmul_mx(
-                    out=acc[:],
+                    out=h_banks[t][half][:],
                     lhsT=w1_q[g, t][0].bitcast(FP8X4),
                     lhsT_scale=w1_q[g, t][1],
-                    rhs=x_q[g, first][0].bitcast(FP8X4),
-                    rhs_scale=x_q[g, first][1],
+                    rhs=x_q[g, half][0][:].bitcast(FP8X4),
+                    rhs_scale=x_q[g, half][1][:],
                     start=(g == 0),
                     stop=(g == 1),
                 )
 
-        def open_hidden(t):
-            banks = [bank([P, count], slot) for (first, count), slot in zip(spans, h_banks[t])]
-            product(t, 0, banks)
-            return banks
-
-        def close_hidden(t, banks):
-            product(t, 1, banks)
-            for (first, count), acc in zip(spans, banks):
-                if t == 0 and first == spans[1][0]:
-                    nc.vector.tensor_scalar_max(h[t][:, first : first + count], acc[:], 0.0)
+        for t in range(PACK):
+            for g in range(2):
+                product(t, g)
+        for t in range(PACK):
+            for half in range(2):
+                dst = h[t][:, HALF * half : HALF * (half + 1)]
+                if t == 0 and half == 0:
+                    nc.vector.tensor_scalar_max(dst, h_banks[t][half][:], 0.0)
                 else:
-                    nc.scalar.activation(h[t][:, first : first + count], acc[:], ACT.Relu)
+                    nc.scalar.activation(dst, h_banks[t][half][:], ACT.Relu)
 
-        banks0 = open_hidden(0)
-        close_hidden(0, banks0)
-        banks1 = open_hidden(1)
-        second1 = sb([P, 1, P, PACK], BF16, "w1g_second1")
-        nc.scalar.copy(*w1_views(second1, 1, 1, 1))
-        quantise_w1(second1, 1, 1, 1)
-        quantise_w1(rest0, 0, 2, 2, "w1g_lead1")
-        rest1 = sb([P, 2, P, PACK], BF16, "w1g_rest1", "w1q1_0_codes")
-        nc.scalar.copy(*w1_views(rest1, 1, 2, 2))
-        close_hidden(1, banks1)
-        quantise_w1(rest1, 1, 2, 2)
-        for t in (2, 3):
-            close_hidden(t, open_hidden(t))
+        sums = [[bank([P, 2, 2, P], 2 * u + vh) for vh in range(2)] for u in range(2)]
+        z_pairs = [[sb([P, 2, P, 2], BF16, "z_pairs%d_%d" % (u, vh)) for vh in range(2)] for u in range(2)]
+        back = [bank([P, 2, 256], 4 + vh) for vh in range(2)]
 
-        z_low = sb([P, 4, P, 2], BF16, "z_low")
-        z_high = [sb([P, 2, P, 2], BF16, "z_high%d" % vh) for vh in range(2)]
-        back = [bank([P, 2, 256], "back%d" % vh) for vh in range(2)]
-
-        def add_neighbours(t, first, blocks, slot):
-            total = bank([P, blocks, P], slot)
-            name = "got%d_%d" % (t, first)
-            halves = [sb([P, 2, P * blocks], F32, name + "_low"), sb([P, 2, P * blocks], F32, name + "_high", "w1raw1" if t == 0 else None)]
-            for d in range(4):
-                got = halves[d // 2][:, d % 2]
-                nc.vector.tensor_copy(got, h[t][:].indirect(entries(pos_t[d], P * first, P * blocks)))
-                for b in range(blocks):
+        def neighbours(t, order):
+            u, e = divmod(t, 2)
+            for place, d in enumerate(order):
+                got = sb([P, V], F32, "got%d_%d" % (t, d))
+                gather(d < VECTOR_LISTS[t], got[:], h[t][:], pos_t[d][:])
+                for c in range(4):
+                    vh, b = divmod(c, 2)
                     nc.tensor.matmul(
-                        total[:, b, :], got[:, P * b : P * (b + 1)], ident[:],
-                        start=(d == 0 and b == 0), stop=(d == 3 and b == blocks - 1), is_transpose=True,
+                        sums[u][vh][:, e, b, :], got[:, P * c : P * (c + 1)], ident[:],
+                        start=(place == 0 and b == 0), stop=(place == 3 and b == 1), is_transpose=True,
                     )
-            return total
 
-        def mean(dst, e, total):
-            nc.scalar.activation(dst[:, :, :, e], total, ACT.Copy, scale=0.25)
+        def mean(u, vh):
+            nc.scalar.activation(z_pairs[u][vh][:], sums[u][vh][:].rearrange("v e b p -> v b p e"), ACT.Copy, scale=0.25)
 
-        def turn_back(src, u, first, blocks):
-            words = src[:].rearrange("v b p e -> v (b p e)").bitcast(F32)
-            for b in range(blocks):
-                c = first + b
-                nc.tensor.transpose(back[c // 2][:, u, P * (c % 2) : P * (c % 2 + 1)], words[:, P * b : P * (b + 1)], ident[:])
+        def turn_back(u, vh):
+            words = z_pairs[u][vh][:].rearrange("v b p e -> v (b p e)").bitcast(F32)
+            for b in range(2):
+                nc.tensor.transpose(back[vh][:, u, P * b : P * (b + 1)], words[:, P * b : P * (b + 1)], ident[:])
 
         def group_z(vh):
             tile = sb([P, 256 * PACK], BF16, "zg%d" % vh)
             nc.scalar.copy(tile[:].bitcast(F32).rearrange("p (v u) -> p v u", u=2), back[vh][:].rearrange("p u v -> p v u"))
             return tile
 
-        for t in range(2):
-            mean(z_low, t, add_neighbours(t, 0, 4, "sum%d" % t)[:])
-        turn_back(z_low, 0, 0, 4)
-        total = add_neighbours(2, 0, 4, "sum0")
+        neighbours(0, (0, 1, 2, 3))
+        neighbours(1, (2, 0, 3, 1))
+        neighbours(2, (2, 3, 0, 1))
+        neighbours(3, (1, 2, 0, 3))
         for vh in range(2):
-            mean(z_high[vh], 0, total[:, 2 * vh : 2 * vh + 2, :])
-        z_grouped = []
+            mean(0, vh)
+
+        stage = [sb([P, PACK, 256], BF16, "c_stage%d" % vh, slot) for vh, slot in enumerate(("got2_2", "got3_1"))]
+        c_grouped = [sb([P, 256, PACK], BF16, "c_grouped%d" % vh, slot) for vh, slot in enumerate((None, "zg0"))]
+
+        def centres(vh, on_vector, tiles):
+            for t in tiles:
+                gather(on_vector, stage[vh][:, t, :], h[t][:], entries(cen_t, 256 * vh, 256))
+
+        centres(0, True, range(PACK))
+        centres(1, True, (0, 1, 2))
         for vh in range(2):
-            total = add_neighbours(3, 2 * vh, 2, "sum%d" % (1 - vh))
-            mean(z_high[vh], 1, total[:])
-            turn_back(z_high[vh], 1, 2 * vh, 2)
-            z_grouped.append(group_z(vh))
-
-        def stage_centres(first, count, slot=None):
-            stage = sb([P, PACK, count], BF16, "c_stage%d" % first, slot)
-            for t in range(PACK):
-                nc.vector.tensor_copy(stage[:, t, :], h[t][:].indirect(entries(cen_t, first, count)))
-            return stage
-
-        def weave(stage, first, count, slot=None):
-            tile = sb([P, count, PACK], BF16, "c_grouped%d" % first, slot)
-            nc.scalar.copy(tile[:].rearrange("p (c i) j -> p c j i", i=4), stage[:].rearrange("p j (c i) -> p c j i", i=4))
-            return tile
-
-        stage01 = stage_centres(0, 256, "got3_0_high")
+            mean(1, vh)
+        for vh in range(2):
+            for u in range(2):
+                turn_back(u, vh)
+        z_grouped = [group_z(vh) for vh in range(2)]
+        centres(1, False, (3,))
+        weave(c_grouped[0][:], stage[0][:], 0, PACK)
         z_q = [quantise(z_grouped[0][:], "zq0")]
-        stage2 = stage_centres(256, P, "got3_2_high")
-        c01 = weave(stage01, 0, 256, "z_high1")
-        c2 = weave(stage2, 256, P, "got3_0_high")
+        c_q = [quantise(flat(c_grouped[0]), "cq0")]
+        weave(c_grouped[1][:], stage[1][:], 0, PACK)
         z_q.append(quantise(z_grouped[1][:], "zq1"))
-        c_q = [quantise(flat(c01), "cq0")]
-        c_q.append(quantise(flat(c2), "cq2"))
-        tail = sb([P, P, PACK], BF16, "c_tail", "got3_2_high")
-        for t in range(PACK):
-            nc.vector.tensor_copy(tail[:, :, t], h[t][:].indirect(entries(cen_t, 3 * P, P)))
-        c_q.append(quantise(flat(tail), "cq3"))
+        c_q.append(quantise(flat(c_grouped[1]), "cq1"))
 
-        def operand(pair, first):
-            return pair[0][:, first : first + P].bitcast(FP8X4), pair[1][:, first : first + P]
-
-        z_ops = [operand(z_q[c // 2], P * (c % 2)) for c in range(4)]
-        c_ops = [operand(c_q[0], 0), operand(c_q[0], P), operand(c_q[1], 0), operand(c_q[2], 0)]
-
-        def last_pass(dst, which, mh, ops):
+        def last_pass(dst, which, mh, ops, start):
             wt, st = last_w[which]
             nc.tensor.matmul_mx(
                 out=dst,
                 lhsT=wt[:, 2 * P * mh : 2 * P * (mh + 1)].bitcast(FP4X4),
                 lhsT_scale=st[:, P * mh : P * (mh + 1)],
-                rhs=ops[0],
-                rhs_scale=ops[1],
-                start=(which == 0),
-                stop=(which == 1),
+                rhs=ops[0][:].bitcast(FP8X4),
+                rhs_scale=ops[1][:],
+                start=start,
+                stop=not start,
             )
 
         out_v = out.rearrange("(a p) v -> p a v", p=P)
-        early = [bank([P, 2 * P], "acc%d" % mh) for mh in range(2)]
-        middle = [bank([P, P], "acc%d" % (2 + mh)) for mh in range(2)]
-        late = [bank([P, P], "sum%d" % mh) for mh in range(2)]
+        early = bank([P, 2, 256], 6)
+        late = [bank([P, 256], slot) for slot in (7, 0)]
         for mh in range(2):
-            for c in range(2):
-                last_pass(early[mh][:, P * c : P * (c + 1)], 0, mh, z_ops[c])
-                last_pass(early[mh][:, P * c : P * (c + 1)], 1, mh, c_ops[c])
+            last_pass(early[:, mh, :], 0, mh, z_q[0], True)
+            last_pass(early[:, mh, :], 1, mh, c_q[0], False)
         for mh in range(2):
-            last_pass(middle[mh][:], 0, mh, z_ops[2])
-            last_pass(late[mh][:], 0, mh, z_ops[3])
-        res_early = sb([P, 2, 3 * P], F32, "res_early")
+            last_pass(late[mh][:], 0, mh, z_q[1], True)
         for mh in range(2):
-            nc.scalar.copy(res_early[:, mh, 0 : 2 * P], early[mh][:])
-        for mh in range(2):
-            last_pass(middle[mh][:], 1, mh, c_ops[2])
-        for mh in range(2):
-            last_pass(late[mh][:], 1, mh, c_ops[3])
-        for mh in range(2):
-            nc.scalar.copy(res_early[:, mh, 2 * P : 3 * P], middle[mh][:])
-        nc.sync.dma_start(out=out_v[:, :, 0 : 3 * P], in_=res_early[:])
-        res_late = sb([P, 2, P], F32, "res_late")
+            last_pass(late[mh][:], 1, mh, c_q[1], False)
+        res_early = sb([P, 2, 256], F32, "res_early")
+        nc.scalar.copy(res_early[:], early[:])
+        nc.sync.dma_start(out=out_v[:, :, 0:256], in_=res_early[:])
+        res_late = sb([P, 2, 256], F32, "res_late")
         nc.scalar.copy(res_late[:, 0, :], late[0][:])
         nc.vector.tensor_copy(res_late[:, 1, :], late[1][:])
-        nc.sync.dma_start(out=out_v[:, :, 3 * P : V], in_=res_late[:])
+        nc.sync.dma_start(out=out_v[:, :, 256:V], in_=res_late[:])

@@ -20,8 +20,9 @@ P = 128
 PACK = 4
 HALF = 512
 
-VECTOR_ENTRIES = (0, 1024, 0, 768, 0, 512, 256, 256)
-VECTOR_LISTS = (4, 2, 2, 1)
+VECTOR_ENTRIES = (0, 1024, 0, 768, 0, 512, 256, 128)
+LAST_PIECES = ((0, 128), (128, 192), (320, 192), (512, 256), (768, 256))
+VECTOR_LISTS = (3, 2, 2, 2)
 
 
 def tile_picked_sagecat_mean_e_kernel(tc, xT, w1, w2_words, w2_scales, w3_words, w3_scales, offs, cen, pos1, pos2, pos3, pos4, out):
@@ -115,8 +116,8 @@ def tile_picked_sagecat_mean_e_kernel(tc, xT, w1, w2_words, w2_scales, w3_words,
             if cut > 0:
                 pick(plane, True, 0, cut)
             if last:
-                for first in range(cut, S, 256):
-                    pick(plane, False, first, 256)
+                for first, count in LAST_PIECES[1:]:
+                    pick(plane, False, first, count)
             elif cut < S:
                 pick(plane, False, cut, S - cut)
             if plane == 1:
@@ -131,72 +132,90 @@ def tile_picked_sagecat_mean_e_kernel(tc, xT, w1, w2_words, w2_scales, w3_words,
             if plane == 5:
                 for half in range(2):
                     weave_x(1, HALF * half, HALF, 0, 2)
-        for first in range(0, S, 256):
-            weave_x(1, first, 256, 2, 2)
+        for first, count in LAST_PIECES[:-1]:
+            weave_x(1, first, count, 2, 2)
+        x_q[1, 0] = quantise(flat(x_grouped[1][0]), "xq1_0")
+        weave_x(1, *LAST_PIECES[-1], 2, 2)
 
         w1_q = {}
 
-        def deal_w1(g, cut):
-            tile = sb([P, PACK, P, PACK], BF16, "w1g%d" % g)
-            src = w1_raw[g][:].rearrange("p j (m t) -> p m j t", t=PACK)
+        def deal_w1(g, pair, on_vector):
+            tile = sb([P, 2, P, PACK], BF16, "w1g%d_%d" % (g, pair))
+            src = w1_raw[g][:].rearrange("p j (m t) -> p m j t", t=PACK)[:, :, :, 2 * pair : 2 * pair + 2]
             dst = tile[:].rearrange("p t m j -> p m j t")
-            nc.scalar.activation(dst[:, cut:P], src[:, cut:P], ACT.Copy)
-            nc.vector.tensor_copy(dst[:, 0:cut], src[:, 0:cut])
+            if on_vector:
+                nc.vector.tensor_copy(dst, src)
+            else:
+                nc.scalar.activation(dst, src, ACT.Copy)
             return tile
 
         def quantise_w1(tile, g, first, count, slot=None):
-            codes, scales = quantise(tile[:, first : first + count].rearrange("p t m j -> p (t m j)"), "w1q%d_%d" % (g, first), slot)
+            part = tile[:, first % 2 : first % 2 + count]
+            codes, scales = quantise(part.rearrange("p t m j -> p (t m j)"), "w1q%d_%d" % (g, first), slot)
             for e in range(count):
                 w1_q[g, first + e] = (codes[:, P * e : P * (e + 1)], scales[:, P * e : P * (e + 1)])
 
-        x_q[1, 0] = quantise(flat(x_grouped[1][0]), "xq1_0")
-        dealt0 = deal_w1(0, 32)
+        low0 = deal_w1(0, 0, False)
+        high0 = deal_w1(0, 1, False)
+        quantise_w1(low0, 0, 0, 1)
         x_q[1, 1] = quantise(flat(x_grouped[1][1]), "xq1_1")
-        quantise_w1(dealt0, 0, 0, 1)
-        dealt1 = deal_w1(1, 70)
-        quantise_w1(dealt1, 1, 0, 1)
-        quantise_w1(dealt0, 0, 1, 3, "w1raw1")
-        quantise_w1(dealt1, 1, 1, 3)
+        low1 = deal_w1(1, 0, True)
+        high1 = deal_w1(1, 1, False)
+        quantise_w1(low1, 1, 0, 2)
+        quantise_w1(low0, 0, 1, 1, "w1g1_0")
+        quantise_w1(high0, 0, 2, 2, "w1g0_0")
+        quantise_w1(high1, 1, 2, 2)
 
         h = [sb([P, S], F32, "h%d" % t) for t in range(PACK)]
-        h_banks = [[bank([P, HALF], 2 * t + half) for half in range(2)] for t in range(PACK)]
+        stretches = (
+            ((0, HALF, 0), (HALF, 256, 1), (768, 256, 2)),
+            ((0, HALF, 3), (HALF, HALF, 4)),
+            ((0, HALF, 5), (HALF, HALF, 6)),
+            ((0, HALF, 7), (HALF, HALF, 2)),
+        )
+        got = {}
 
-        def product(t, g):
-            for half in range(2):
-                nc.tensor.matmul_mx(
-                    out=h_banks[t][half][:],
-                    lhsT=w1_q[g, t][0].bitcast(FP8X4),
-                    lhsT_scale=w1_q[g, t][1],
-                    rhs=x_q[g, half][0][:].bitcast(FP8X4),
-                    rhs_scale=x_q[g, half][1][:],
-                    start=(g == 0),
-                    stop=(g == 1),
-                )
+        def neighbours(t):
+            for d in range(4):
+                got[t, d] = sb([P, V], F32, "got%d_%d" % (t, d))
+                gather(d < VECTOR_LISTS[t], got[t, d][:], h[t][:], pos_t[d][:])
 
         for t in range(PACK):
+            accs = [bank([P, count], slot) for first, count, slot in stretches[t]]
             for g in range(2):
-                product(t, g)
-        for t in range(PACK):
-            for half in range(2):
-                dst = h[t][:, HALF * half : HALF * (half + 1)]
-                if t == 0 and half == 0:
-                    nc.vector.tensor_scalar_max(dst, h_banks[t][half][:], 0.0)
+                for (first, count, slot), acc in zip(stretches[t], accs):
+                    half, at = divmod(first, HALF)
+                    nc.tensor.matmul_mx(
+                        out=acc[:],
+                        lhsT=w1_q[g, t][0].bitcast(FP8X4),
+                        lhsT_scale=w1_q[g, t][1],
+                        rhs=x_q[g, half][0][:, at : at + count].bitcast(FP8X4),
+                        rhs_scale=x_q[g, half][1][:, at : at + count],
+                        start=(g == 0),
+                        stop=(g == 1),
+                    )
+            for (first, count, slot), acc in zip(stretches[t], accs):
+                dst = h[t][:, first : first + count]
+                if t == 0 and first == 0:
+                    nc.vector.tensor_scalar_max(dst, acc[:], 0.0)
                 else:
-                    nc.scalar.activation(dst, h_banks[t][half][:], ACT.Relu)
+                    nc.scalar.activation(dst, acc[:], ACT.Relu)
+            if t == 0:
+                neighbours(0)
+        for t in range(1, PACK):
+            neighbours(t)
 
-        sums = [[bank([P, 2, 2, P], 2 * u + vh) for vh in range(2)] for u in range(2)]
+        sums = [[bank([P, 2, 2, P], 3 * u + vh) for vh in range(2)] for u in range(2)]
         z_pairs = [[sb([P, 2, P, 2], BF16, "z_pairs%d_%d" % (u, vh)) for vh in range(2)] for u in range(2)]
-        back = [bank([P, 2, 256], 4 + vh) for vh in range(2)]
+        back = [bank([P, 2, 256], 5 + vh) for vh in range(2)]
 
-        def neighbours(t, order):
+        def add_up(t, order):
             u, e = divmod(t, 2)
             for place, d in enumerate(order):
-                got = sb([P, V], F32, "got%d_%d" % (t, d))
-                gather(d < VECTOR_LISTS[t], got[:], h[t][:], pos_t[d][:])
                 for c in range(4):
                     vh, b = divmod(c, 2)
                     nc.tensor.matmul(
-                        sums[u][vh][:, e, b, :], got[:, P * c : P * (c + 1)], ident[:],
+                        sums[u][vh][:, e, b, :], got[t, d][:, P * c : P * (c + 1)], ident[:],
                         start=(place == 0 and b == 0), stop=(place == 3 and b == 1), is_transpose=True,
                     )
 
@@ -213,62 +232,76 @@ def tile_picked_sagecat_mean_e_kernel(tc, xT, w1, w2_words, w2_scales, w3_words,
             nc.scalar.copy(tile[:].bitcast(F32).rearrange("p (v u) -> p v u", u=2), back[vh][:].rearrange("p u v -> p v u"))
             return tile
 
-        neighbours(0, (0, 1, 2, 3))
-        neighbours(1, (2, 0, 3, 1))
-        neighbours(2, (2, 3, 0, 1))
-        neighbours(3, (1, 2, 0, 3))
+        add_up(0, (0, 3, 1, 2))
+        for t in range(1, PACK):
+            add_up(t, (0, 1, 2, 3))
         for vh in range(2):
             mean(0, vh)
 
-        stage = [sb([P, PACK, 256], BF16, "c_stage%d" % vh, slot) for vh, slot in enumerate(("got2_2", "got3_1"))]
-        c_grouped = [sb([P, 256, PACK], BF16, "c_grouped%d" % vh, slot) for vh, slot in enumerate((None, "zg0"))]
+        c_blocks = ((0, 256), (256, P), (384, P))
+        stage = [sb([P, PACK, count], BF16, "c_stage%d" % first, slot) for (first, count), slot in zip(c_blocks, ("got2_0", "got2_1", "z_pairs1_1"))]
+        c_grouped = [sb([P, count, PACK], BF16, "c_grouped%d" % first) for first, count in c_blocks]
 
-        def centres(vh, on_vector, tiles):
+        def centres(block, on_vector, tiles):
             for t in tiles:
-                gather(on_vector, stage[vh][:, t, :], h[t][:], entries(cen_t, 256 * vh, 256))
+                gather(on_vector, stage[block][:, t, :], h[t][:], entries(cen_t, *c_blocks[block]))
 
-        centres(0, True, range(PACK))
-        centres(1, True, (0, 1, 2))
         for vh in range(2):
             mean(1, vh)
         for vh in range(2):
             for u in range(2):
                 turn_back(u, vh)
         z_grouped = [group_z(vh) for vh in range(2)]
-        centres(1, False, (3,))
+        centres(0, True, range(PACK))
+        centres(1, True, (0, 1))
         weave(c_grouped[0][:], stage[0][:], 0, PACK)
-        z_q = [quantise(z_grouped[0][:], "zq0")]
+        centres(1, True, (2, 3))
         c_q = [quantise(flat(c_grouped[0]), "cq0")]
         weave(c_grouped[1][:], stage[1][:], 0, PACK)
-        z_q.append(quantise(z_grouped[1][:], "zq1"))
         c_q.append(quantise(flat(c_grouped[1]), "cq1"))
+        z_q = [quantise(z_grouped[0][:], "zq0")]
+        z_q.append(quantise(z_grouped[1][:], "zq1"))
+        centres(2, False, range(PACK))
+        weave(c_grouped[2][:], stage[2][:], 0, PACK)
+        c_q.append(quantise(flat(c_grouped[2]), "cq2"))
 
-        def last_pass(dst, which, mh, ops, start):
+        def last_pass(dst, which, mh, ops, start, stop):
             wt, st = last_w[which]
             nc.tensor.matmul_mx(
                 out=dst,
                 lhsT=wt[:, 2 * P * mh : 2 * P * (mh + 1)].bitcast(FP4X4),
                 lhsT_scale=st[:, P * mh : P * (mh + 1)],
-                rhs=ops[0][:].bitcast(FP8X4),
-                rhs_scale=ops[1][:],
+                rhs=ops[0].bitcast(FP8X4),
+                rhs_scale=ops[1],
                 start=start,
-                stop=not start,
+                stop=stop,
             )
 
+        def columns(pair, first, count):
+            return pair[0][:, first : first + count], pair[1][:, first : first + count]
+
         out_v = out.rearrange("(a p) v -> p a v", p=P)
-        early = bank([P, 2, 256], 6)
-        late = [bank([P, 256], slot) for slot in (7, 0)]
+        early = bank([P, 2, 256], 4)
+        middle = [bank([P, P], slot) for slot in (5, 6)]
+        late = [bank([P, P], slot) for slot in (0, 1)]
         for mh in range(2):
-            last_pass(early[:, mh, :], 0, mh, z_q[0], True)
-            last_pass(early[:, mh, :], 1, mh, c_q[0], False)
+            last_pass(early[:, mh, :], 1, mh, columns(c_q[0], 0, 256), mh == 0, False)
         for mh in range(2):
-            last_pass(late[mh][:], 0, mh, z_q[1], True)
+            last_pass(middle[mh][:], 1, mh, columns(c_q[1], 0, P), True, False)
         for mh in range(2):
-            last_pass(late[mh][:], 1, mh, c_q[1], False)
-        res_early = sb([P, 2, 256], F32, "res_early")
-        nc.scalar.copy(res_early[:], early[:])
-        nc.sync.dma_start(out=out_v[:, :, 0:256], in_=res_early[:])
-        res_late = sb([P, 2, 256], F32, "res_late")
+            last_pass(early[:, mh, :], 0, mh, columns(z_q[0], 0, 256), False, mh == 1)
+        for mh in range(2):
+            last_pass(middle[mh][:], 0, mh, columns(z_q[1], 0, P), False, True)
+        for mh in range(2):
+            last_pass(late[mh][:], 0, mh, columns(z_q[1], P, P), True, False)
+        for mh in range(2):
+            last_pass(late[mh][:], 1, mh, columns(c_q[2], 0, P), False, True)
+        res_early = sb([P, 2, 3 * P], F32, "res_early")
+        nc.scalar.copy(res_early[:, :, 0:256], early[:])
+        nc.scalar.copy(res_early[:, 0, 256 : 3 * P], middle[0][:])
+        nc.vector.tensor_copy(res_early[:, 1, 256 : 3 * P], middle[1][:])
+        nc.sync.dma_start(out=out_v[:, :, 0 : 3 * P], in_=res_early[:])
+        res_late = sb([P, 2, P], F32, "res_late")
         nc.scalar.copy(res_late[:, 0, :], late[0][:])
         nc.vector.tensor_copy(res_late[:, 1, :], late[1][:])
-        nc.sync.dma_start(out=out_v[:, :, 256:V], in_=res_late[:])
+        nc.sync.dma_start(out=out_v[:, :, 3 * P : V], in_=res_late[:])

@@ -23,6 +23,7 @@ HALF = 512
 VECTOR_ENTRIES = (0, 1024, 0, 768, 0, 512, 256, 128)
 LAST_PIECES = ((0, 128), (128, 192), (320, 192), (512, 256), (768, 256))
 VECTOR_LISTS = (3, 2, 2, 2)
+SHARED_LIST = (2, 1)
 
 
 def tile_picked_sagecat_mean_e_kernel(tc, xT, w1, w2_words, w2_scales, w3_words, w3_scales, offs, cen, pos1, pos2, pos3, pos4, out):
@@ -178,7 +179,11 @@ def tile_picked_sagecat_mean_e_kernel(tc, xT, w1, w2_words, w2_scales, w3_words,
         def neighbours(t):
             for d in range(4):
                 got[t, d] = sb([P, V], F32, "got%d_%d" % (t, d))
-                gather(d < VECTOR_LISTS[t], got[t, d][:], h[t][:], pos_t[d][:])
+                if (t, d) == SHARED_LIST:
+                    for vh in range(2):
+                        gather(vh == 0, got[t, d][:, 256 * vh : 256 * (vh + 1)], h[t][:], entries(pos_t[d], 256 * vh, 256))
+                else:
+                    gather(d < VECTOR_LISTS[t], got[t, d][:], h[t][:], pos_t[d][:])
 
         for t in range(PACK):
             accs = [bank([P, count], slot) for first, count, slot in stretches[t]]

@@ -156,6 +156,18 @@ def tile_picked_sagecat_mean_e_kernel(tc, xT, w1, w2_words, w2_scales, w3_words,
             for e in range(count):
                 w1_q[g, first + e] = (codes[:, P * e : P * (e + 1)], scales[:, P * e : P * (e + 1)])
 
+        idle = bank([P, HALF], 7)
+        for start in (True, False):
+            nc.tensor.matmul_mx(
+                out=idle[:],
+                lhsT=x_q[1, 0][0][:, 0:P].bitcast(FP8X4),
+                lhsT_scale=x_q[1, 0][1][:, 0:P],
+                rhs=x_q[1, 0][0][:].bitcast(FP8X4),
+                rhs_scale=x_q[1, 0][1][:],
+                start=start,
+                stop=not start,
+            )
+
         low0 = deal_w1(0, 0, False)
         high0 = deal_w1(0, 1, False)
         quantise_w1(low0, 0, 0, 1)

@@ -256,8 +256,8 @@ def tile_picked_sagecat_mean_e_kernel(tc, xT, w1, w2_words, w2_scales, w3_words,
             mean(0, vh)
 
         c_blocks = ((0, 256), (256, P), (384, P))
-        stage = [sb([P, PACK, count], BF16, "c_stage%d" % first, slot) for (first, count), slot in zip(c_blocks, ("got2_0", "got2_1", "z_pairs1_1"))]
-        c_grouped = [sb([P, count, PACK], BF16, "c_grouped%d" % first) for first, count in c_blocks]
+        stage = [sb([P, PACK, count], BF16, "c_stage%d" % first, slot) for (first, count), slot in zip(c_blocks, ("got2_0", "got2_1", "z_pairs1_0"))]
+        c_grouped = {0: sb([P, 256, PACK], BF16, "c_grouped0"), 2: sb([P, P, PACK], BF16, "c_grouped384")}
 
         def centres(block, on_vector, tiles):
             for t in tiles:
@@ -274,9 +274,10 @@ def tile_picked_sagecat_mean_e_kernel(tc, xT, w1, w2_words, w2_scales, w3_words,
         weave(c_grouped[0][:], stage[0][:], 0, PACK)
         centres(1, True, (2, 3))
         c_q = [quantise(flat(c_grouped[0]), "cq0")]
+        c_grouped[1] = sb([P, P, PACK], BF16, "c_grouped256", "z_pairs1_1")
         weave(c_grouped[1][:], stage[1][:], 0, PACK)
-        c_q.append(quantise(flat(c_grouped[1]), "cq1"))
         z_q = [quantise(z_grouped[0][:], "zq0")]
+        c_q.append(quantise(flat(c_grouped[1]), "cq1"))
         z_q.append(quantise(z_grouped[1][:], "zq1"))
         centres(2, False, range(PACK))
         weave(c_grouped[2][:], stage[2][:], 0, PACK)
@@ -304,9 +305,9 @@ def tile_picked_sagecat_mean_e_kernel(tc, xT, w1, w2_words, w2_scales, w3_words,
         for mh in range(2):
             last_pass(early[:, mh, :], 1, mh, columns(c_q[0], 0, 256), mh == 0, False)
         for mh in range(2):
-            last_pass(middle[mh][:], 1, mh, columns(c_q[1], 0, P), True, False)
-        for mh in range(2):
             last_pass(early[:, mh, :], 0, mh, columns(z_q[0], 0, 256), False, mh == 1)
+        for mh in range(2):
+            last_pass(middle[mh][:], 1, mh, columns(c_q[1], 0, P), True, False)
         for mh in range(2):
             last_pass(middle[mh][:], 0, mh, columns(z_q[1], 0, P), False, True)
         for mh in range(2):

@@ -20,7 +20,7 @@ P = 128
 PACK = 4
 HALF = 512
 
-VECTOR_ENTRIES = (0, 1024, 0, 768, 0, 512, 256, 128)
+VECTOR_ENTRIES = (0, 1024, 0, 640, 0, 512, 256, 128)
 LAST_PIECES = ((0, 128), (128, 192), (320, 192), (512, 256), (768, 256))
 VECTOR_LISTS = (3, 2, 2, 2)
 SHARED_LIST = (2, 1)
@@ -140,21 +140,18 @@ def tile_picked_sagecat_mean_e_kernel(tc, xT, w1, w2_words, w2_scales, w3_words,
 
         w1_q = {}
 
-        def deal_w1(g, pair, on_vector):
-            tile = sb([P, 2, P, PACK], BF16, "w1g%d_%d" % (g, pair))
-            src = w1_raw[g][:].rearrange("p j (m t) -> p m j t", t=PACK)[:, :, :, 2 * pair : 2 * pair + 2]
-            dst = tile[:].rearrange("p t m j -> p m j t")
+        def deal_w1(tile, g, pair, first, count, on_vector):
+            src = w1_raw[g][:].rearrange("p j (m t) -> p m j t", t=PACK)[:, first : first + count, :, 2 * pair : 2 * pair + 2]
+            dst = tile.rearrange("p t m j -> p m j t")[:, first : first + count]
             if on_vector:
                 nc.vector.tensor_copy(dst, src)
             else:
                 nc.scalar.activation(dst, src, ACT.Copy)
-            return tile
 
-        def quantise_w1(tile, g, first, count, slot=None):
-            part = tile[:, first % 2 : first % 2 + count]
-            codes, scales = quantise(part.rearrange("p t m j -> p (t m j)"), "w1q%d_%d" % (g, first), slot)
-            for e in range(count):
-                w1_q[g, first + e] = (codes[:, P * e : P * (e + 1)], scales[:, P * e : P * (e + 1)])
+        def quantise_w1(part, name, places, slot=None):
+            codes, scales = quantise(part, name, slot)
+            for e, place in enumerate(places):
+                w1_q[place] = (codes[:, P * e : P * (e + 1)], scales[:, P * e : P * (e + 1)])
 
         idle = bank([P, HALF], 7)
         for start in (True, False):
@@ -168,16 +165,18 @@ def tile_picked_sagecat_mean_e_kernel(tc, xT, w1, w2_words, w2_scales, w3_words,
                 stop=not start,
             )
 
-        low0 = deal_w1(0, 0, False)
-        high0 = deal_w1(0, 1, False)
-        quantise_w1(low0, 0, 0, 1)
+        low = [sb([P, 2, P, PACK], BF16, "w1low%d" % g) for g in range(2)]
+        high = sb([P, 2, 2, P, PACK], BF16, "w1high")
+        deal_w1(low[0][:], 0, 0, 0, P, False)
+        deal_w1(high[:, 0], 0, 1, 0, P, False)
+        quantise_w1(low[0][:, 0].rearrange("p m j -> p (m j)"), "w1q_first", [(0, 0)])
         x_q[1, 1] = quantise(flat(x_grouped[1][1]), "xq1_1")
-        low1 = deal_w1(1, 0, True)
-        high1 = deal_w1(1, 1, False)
-        quantise_w1(low1, 1, 0, 2)
-        quantise_w1(low0, 0, 1, 1, "w1g1_0")
-        quantise_w1(high0, 0, 2, 2, "w1g0_0")
-        quantise_w1(high1, 1, 2, 2)
+        deal_w1(low[1][:], 1, 0, 0, P, True)
+        deal_w1(high[:, 1], 1, 1, 0, 64, True)
+        deal_w1(high[:, 1], 1, 1, 64, 64, False)
+        quantise_w1(low[1][:].rearrange("p t m j -> p (t m j)"), "w1q_low", [(1, 0), (1, 1)])
+        quantise_w1(low[0][:, 1].rearrange("p m j -> p (m j)"), "w1q_second", [(0, 1)], "w1low1")
+        quantise_w1(high[:].rearrange("p g t m j -> p (g t m j)"), "w1q_high", [(0, 2), (0, 3), (1, 2), (1, 3)])
 
         h = [sb([P, S], F32, "h%d" % t) for t in range(PACK)]
         stretches = (
@@ -213,7 +212,7 @@ def tile_picked_sagecat_mean_e_kernel(tc, xT, w1, w2_words, w2_scales, w3_words,
                     )
             for (first, count, slot), acc in zip(stretches[t], accs):
                 dst = h[t][:, first : first + count]
-                if t == 0 and first == 0:
+                if t == 0 and first == 768:
                     nc.vector.tensor_scalar_max(dst, acc[:], 0.0)
                 else:
                     nc.scalar.activation(dst, acc[:], ACT.Relu)

from contextlib import ExitStack

import concourse.mybir as mybir
from concourse.masks import make_identity

K, T, S, V, H, N = 1024, 2048, 1024, 512, 512, 256
FLOPS = 2 * K * H * S + 2 * 2 * H * N * V

F32 = mybir.dt.float32
BF16 = mybir.dt.bfloat16
I32 = mybir.dt.int32
U32 = mybir.dt.uint32
U16 = mybir.dt.uint16
U8 = mybir.dt.uint8
FP8X4 = mybir.dt.float8_e4m3fn_x4
FP4X4 = mybir.dt.float4_e2m1fn_x4
ACT = mybir.ActivationFunctionType

P = 128
PACK = 4
HALF = 512

VECTOR_ENTRIES = (0, 1024, 0, 640, 0, 512, 256, 128)
LAST_PIECES = ((0, 128), (128, 192), (320, 192), (512, 256), (768, 256))
VECTOR_LISTS = (3, 2, 2, 2)
SHARED_LIST = (2, 1)


def tile_picked_sagecat_mean_e_kernel(tc, xT, w1, w2_words, w2_scales, w3_words, w3_scales, offs, cen, pos1, pos2, pos3, pos4, out):
    nc = tc.nc
    with ExitStack() as ctx:
        lists = ctx.enter_context(tc.tile_pool(name="lists", bufs=1))
        keep = ctx.enter_context(tc.tile_pool(name="keep", bufs=1))
        psum = ctx.enter_context(tc.psum_pool(name="psum", bufs=1))

        def sb(shape, dtype, name, slot=None):
            return keep.tile(shape, dtype, name=name, tag=slot or name, align_bytes=64)

        def bank(shape, slot):
            return psum.tile(shape, F32, name="bank%d" % slot)

        def entries(tile, first, count):
            return tile[:, first // 16 : (first + count) // 16]

        def gather(on_vector, dst, window, offsets):
            if on_vector:
                nc.vector.tensor_copy(dst, window.indirect(offsets))
            else:
                nc.scalar.activation(dst, window.indirect(offsets), ACT.Copy)

        def quantise(grouped, name, slot=None):
            width = grouped.shape[1] // PACK
            codes = sb([P, width], U32, name + "_codes", slot)
            scales = sb([P, width], U8, name + "_scales")
            nc.vector.quantize_mx(out=codes[:].bitcast(FP8X4), scales=scales[:], in_=grouped)
            return codes, scales

        def weave(grouped, planes, first, count, on_vector=True):
            dst = grouped.rearrange("p (c i) j -> p c j i", i=4)[:, :, first : first + count]
            src = planes.rearrange("p j (c i) -> p c j i", i=4)[:, :, first : first + count]
            if on_vector:
                nc.vector.tensor_copy(dst, src)
            else:
                nc.scalar.activation(dst, src, ACT.Copy)

        def flat(tile):
            return tile[:].rearrange("p n j -> p (n j)")

        def load_list(src, name):
            tile = lists.tile([P, src.shape[1]], U16, name=name)
            nc.sync.dma_start(tile[:], src)
            return tile

        x_raw = []
        for plane in range(2 * PACK):
            g, j = divmod(plane, PACK)
            tile = sb([P, T], F32, "x%d" % plane)
            rows = xT[512 * g : 512 * (g + 1), :].rearrange("(p j) t -> p j t", j=PACK)
            nc.sync.dma_start(out=tile[:], in_=rows[:, j, :])
            x_raw.append(tile)
            if plane == 0:
                offs_t = load_list(offs, "offs")
        w1_raw = [sb([P, PACK, H], F32, "w1raw%d" % g) for g in range(2)]
        for g in range(2):
            nc.sync.dma_start(out=w1_raw[g][:], in_=w1[512 * g : 512 * (g + 1), :].rearrange("(p j) c -> p j c", j=PACK))
        pos_t = [load_list(src, "pos%d" % d) for d, src in enumerate((pos1, pos2, pos3, pos4))]
        cen_t = load_list(cen, "cen")

        last_w = []
        for name, words in (("w3", w3_words), ("w2", w2_words)):
            wt = sb([P, 2 * N], U8, name + "_words")
            st = sb([P, N], U8, name + "_plane")
            nc.gpsimd.memset(st[:].bitcast(I32), 0)
            nc.sync.dma_start(out=wt[:], in_=words[0])
            last_w.append((wt, st))
        for (wt, st), scales in zip(last_w, (w3_scales, w2_scales)):
            for q in range(4):
                nc.sync.dma_start(out=st[32 * q : 32 * q + 4, :].bitcast(I32), in_=scales[0, 4 * q : 4 * q + 4, :].bitcast(I32))

        ident = sb([P, P], F32, "ident")
        make_identity(nc, ident[:])

        planes = [sb([P, PACK, S], BF16, "planes%d" % g) for g in range(2)]
        x_grouped = [[sb([P, HALF, PACK], BF16, "xg%d_%d" % (g, half)) for half in range(2)] for g in range(2)]
        x_q = {}

        def pick(plane, on_vector, first, count):
            g, j = divmod(plane, PACK)
            gather(on_vector, planes[g][:, j, first : first + count], x_raw[plane][:], entries(offs_t, first, count))

        def weave_x(g, first, count, j_first, j_count, on_vector=True):
            half, at = divmod(first, HALF)
            weave(x_grouped[g][half][:, at : at + count], planes[g][:, :, first : first + count], j_first, j_count, on_vector)

        for plane, cut in enumerate(VECTOR_ENTRIES):
            last = plane == 2 * PACK - 1
            if cut > 0:
                pick(plane, True, 0, cut)
            if last:
                for first, count in LAST_PIECES[1:]:
                    pick(plane, False, first, count)
            elif cut < S:
                pick(plane, False, cut, S - cut)
            if plane == 1:
                weave_x(0, 0, HALF, 0, 2)
                weave_x(0, HALF, HALF - P, 0, 2)
            if plane == 3:
                weave_x(0, 0, HALF, 2, 2)
                weave_x(0, HALF, HALF - P, 2, 2)
                weave_x(0, S - P, P, 0, PACK, False)
                for half in range(2):
                    x_q[0, half] = quantise(flat(x_grouped[0][half]), "xq0_%d" % half)
            if plane == 5:
                for half in range(2):
                    weave_x(1, HALF * half, HALF, 0, 2)
        for first, count in LAST_PIECES[:-1]:
            weave_x(1, first, count, 2, 2)
        x_q[1, 0] = quantise(flat(x_grouped[1][0]), "xq1_0")
        weave_x(1, *LAST_PIECES[-1], 2, 2)

        w1_q = {}

        def deal_w1(tile, g, pair, first, count, on_vector):
            src = w1_raw[g][:].rearrange("p j (m t) -> p m j t", t=PACK)[:, first : first + count, :, 2 * pair : 2 * pair + 2]
            dst = tile.rearrange("p t m j -> p m j t")[:, first : first + count]
            if on_vector:
                nc.vector.tensor_copy(dst, src)
            else:
                nc.scalar.activation(dst, src, ACT.Copy)

        def quantise_w1(part, name, places, slot=None):
            codes, scales = quantise(part, name, slot)
            for e, place in enumerate(places):
                w1_q[place] = (codes[:, P * e : P * (e + 1)], scales[:, P * e : P * (e + 1)])

        idle = bank([P, HALF], 7)
        for start in (True, False):
            nc.tensor.matmul_mx(
                out=idle[:],
                lhsT=x_q[1, 0][0][:, 0:P].bitcast(FP8X4),
                lhsT_scale=x_q[1, 0][1][:, 0:P],
                rhs=x_q[1, 0][0][:].bitcast(FP8X4),
                rhs_scale=x_q[1, 0][1][:],
                start=start,
                stop=not start,
            )

        low = [sb([P, 2, P, PACK], BF16, "w1low%d" % g) for g in range(2)]
        high = sb([P, 2, 2, P, PACK], BF16, "w1high")
        deal_w1(low[0][:], 0, 0, 0, P, False)
        deal_w1(high[:, 0], 0, 1, 0, P, False)
        quantise_w1(low[0][:, 0].rearrange("p m j -> p (m j)"), "w1q_first", [(0, 0)])
        x_q[1, 1] = quantise(flat(x_grouped[1][1]), "xq1_1")
        deal_w1(low[1][:], 1, 0, 0, P, True)
        deal_w1(high[:, 1], 1, 1, 0, 64, True)
        deal_w1(high[:, 1], 1, 1, 64, 64, False)
        quantise_w1(low[1][:].rearrange("p t m j -> p (t m j)"), "w1q_low", [(1, 0), (1, 1)])
        quantise_w1(low[0][:, 1].rearrange("p m j -> p (m j)"), "w1q_second", [(0, 1)], "w1low1")
        quantise_w1(high[:].rearrange("p g t m j -> p (g t m j)"), "w1q_high", [(0, 2), (0, 3), (1, 2), (1, 3)])

        h = [sb([P, S], F32, "h%d" % t) for t in range(PACK)]
        stretches = (
            ((0, HALF, 0), (HALF, 256, 1), (768, 256, 2)),
            ((0, HALF, 3), (HALF, HALF, 4)),
            ((0, HALF, 5), (HALF, HALF, 6)),
            ((0, HALF, 7), (HALF, HALF, 2)),
        )
        got = {}

        def neighbours(t):
            for d in range(4):
                got[t, d] = sb([P, V], F32, "got%d_%d" % (t, d))
                if (t, d) == SHARED_LIST:
                    for vh in range(2):
                        gather(vh == 0, got[t, d][:, 256 * vh : 256 * (vh + 1)], h[t][:], entries(pos_t[d], 256 * vh, 256))
                else:
                    gather(d < VECTOR_LISTS[t], got[t, d][:], h[t][:], pos_t[d][:])

        for t in range(PACK):
            accs = [bank([P, count], slot) for first, count, slot in stretches[t]]
            for g in range(2):
                for (first, count, slot), acc in zip(stretches[t], accs):
                    half, at = divmod(first, HALF)
                    nc.tensor.matmul_mx(
                        out=acc[:],
                        lhsT=w1_q[g, t][0].bitcast(FP8X4),
                        lhsT_scale=w1_q[g, t][1],
                        rhs=x_q[g, half][0][:, at : at + count].bitcast(FP8X4),
                        rhs_scale=x_q[g, half][1][:, at : at + count],
                        start=(g == 0),
                        stop=(g == 1),
                    )
            for (first, count, slot), acc in zip(stretches[t], accs):
                dst = h[t][:, first : first + count]
                if t == 0 and first == 768:
                    nc.vector.tensor_scalar_max(dst, acc[:], 0.0)
                else:
                    nc.scalar.activation(dst, acc[:], ACT.Relu)
            if t == 0:
                neighbours(0)
        for t in range(1, PACK):
            neighbours(t)

        sums = [[bank([P, 2, 2, P], 3 * u + vh) for vh in range(2)] for u in range(2)]
        z_pairs = [[sb([P, 2, P, 2], BF16, "z_pairs%d_%d" % (u, vh)) for vh in range(2)] for u in range(2)]
        back = [bank([P, 2, 256], 5 + vh) for vh in range(2)]

        def add_up(t, order):
            u, e = divmod(t, 2)
            for place, d in enumerate(order):
                for c in range(4):
                    vh, b = divmod(c, 2)
                    nc.tensor.matmul(
                        sums[u][vh][:, e, b, :], got[t, d][:, P * c : P * (c + 1)], ident[:],
                        start=(place == 0 and b == 0), stop=(place == 3 and b == 1), is_transpose=True,
                    )

        def mean(u, vh):
            nc.scalar.activation(z_pairs[u][vh][:], sums[u][vh][:].rearrange("v e b p -> v b p e"), ACT.Copy, scale=0.25)

        def turn_back(u, vh):
            words = z_pairs[u][vh][:].rearrange("v b p e -> v (b p e)").bitcast(F32)
            for b in range(2):
                nc.tensor.transpose(back[vh][:, u, P * b : P * (b + 1)], words[:, P * b : P * (b + 1)], ident[:])

        def group_z(vh):
            tile = sb([P, 256 * PACK], BF16, "zg%d" % vh)
            nc.scalar.copy(tile[:].bitcast(F32).rearrange("p (v u) -> p v u", u=2), back[vh][:].rearrange("p u v -> p v u"))
            return tile

        add_up(0, (0, 3, 1, 2))
        for t in range(1, PACK):
            add_up(t, (0, 1, 2, 3))
        for vh in range(2):
            mean(0, vh)

        c_blocks = ((0, 256), (256, P), (384, P))
        stage = [sb([P, PACK, count], BF16, "c_stage%d" % first, slot) for (first, count), slot in zip(c_blocks, ("got2_0", "got2_1", "z_pairs1_0"))]
        c_grouped = {0: sb([P, 256, PACK], BF16, "c_grouped0"), 2: sb([P, P, PACK], BF16, "c_grouped384")}

        def centres(block, on_vector, tiles):
            for t in tiles:
                gather(on_vector, stage[block][:, t, :], h[t][:], entries(cen_t, *c_blocks[block]))

        for vh in range(2):
            mean(1, vh)
        for vh in range(2):
            for u in range(2):
                turn_back(u, vh)
        z_grouped = [group_z(vh) for vh in range(2)]
        centres(0, True, range(PACK))
        centres(1, True, (0, 1))
        weave(c_grouped[0][:], stage[0][:], 0, PACK)
        centres(1, True, (2, 3))
        c_q = [quantise(flat(c_grouped[0]), "cq0")]
        c_grouped[1] = sb([P, P, PACK], BF16, "c_grouped256", "z_pairs1_1")
        weave(c_grouped[1][:], stage[1][:], 0, PACK)
        z_q = [quantise(z_grouped[0][:], "zq0")]
        c_q.append(quantise(flat(c_grouped[1]), "cq1"))
        z_q.append(quantise(z_grouped[1][:], "zq1"))
        centres(2, False, range(PACK))
        weave(c_grouped[2][:], stage[2][:], 0, PACK)
        c_q.append(quantise(flat(c_grouped[2]), "cq2"))

        def last_pass(dst, which, mh, ops, start, stop):
            wt, st = last_w[which]
            nc.tensor.matmul_mx(
                out=dst,
                lhsT=wt[:, 2 * P * mh : 2 * P * (mh + 1)].bitcast(FP4X4),
                lhsT_scale=st[:, P * mh : P * (mh + 1)],
                rhs=ops[0].bitcast(FP8X4),
                rhs_scale=ops[1],
                start=start,
                stop=stop,
            )

        def columns(pair, first, count):
            return pair[0][:, first : first + count], pair[1][:, first : first + count]

        out_v = out.rearrange("(a p) v -> p a v", p=P)
        early = bank([P, 2, 256], 4)
        middle = [bank([P, P], slot) for slot in (5, 6)]
        late = [bank([P, P], slot) for slot in (0, 1)]
        for mh in range(2):
            last_pass(early[:, mh, :], 1, mh, columns(c_q[0], 0, 256), mh == 0, False)
        for mh in range(2):
            last_pass(early[:, mh, :], 0, mh, columns(z_q[0], 0, 256), False, mh == 1)
        for mh in range(2):
            last_pass(middle[mh][:], 1, mh, columns(c_q[1], 0, P), True, False)
        for mh in range(2):
            last_pass(middle[mh][:], 0, mh, columns(z_q[1], 0, P), False, True)
        for mh in range(2):
            last_pass(late[mh][:], 0, mh, columns(z_q[1], P, P), True, False)
        for mh in range(2):
            last_pass(late[mh][:], 1, mh, columns(c_q[2], 0, P), False, True)
        res_early = sb([P, 2, 3 * P], F32, "res_early")
        nc.scalar.copy(res_early[:, :, 0:256], early[:])
        nc.scalar.copy(res_early[:, 0, 256 : 3 * P], middle[0][:])
        nc.vector.tensor_copy(res_early[:, 1, 256 : 3 * P], middle[1][:])
        nc.sync.dma_start(out=out_v[:, :, 0 : 3 * P], in_=res_early[:])
        res_late = sb([P, 2, P], F32, "res_late")
        nc.scalar.copy(res_late[:, 0, :], late[0][:])
        nc.vector.tensor_copy(res_late[:, 1, :], late[1][:])
        nc.sync.dma_start(out=out_v[:, :, 3 * P : V], in_=res_late[:])
